import numpy as np
import ml_dtypes


def mxq(x, axis, fmt="e4m3"):
    dtype, down = {"e4m3": (ml_dtypes.float8_e4m3fn, 7), "e5m2": (ml_dtypes.float8_e5m2, 14)}[fmt]
    v = np.moveaxis(np.asarray(x, np.float32).astype(ml_dtypes.bfloat16).astype(np.float64), axis, -1)
    blocks = v.reshape(v.shape[:-1] + (-1, 32))
    amax = np.abs(blocks).max(-1, keepdims=True)
    byte = np.maximum(np.where(amax > 0, np.frexp(amax)[1] - 1 + 127, 0) - down, 1)
    scale = np.exp2(byte - 127.0)
    codes = (blocks / scale).astype(np.float32).astype(dtype).astype(np.float64)
    return np.moveaxis((codes * scale).reshape(v.shape), -1, axis)


WIDE = False


def mx_kscale(k):
    if not WIDE:
        return np.ones(k)
    levels = np.array([24, -24, 12, -12, 0])
    if k % 512:
        return np.exp2(np.random.permutation(np.resize(levels, k // 32))).repeat(32)
    a = np.empty((k // 512, 16))
    for p in range(k // 512):
        a[p, :8] = np.random.permutation(np.resize(levels, 8))
        for g in range(8):
            far = levels[np.abs(levels - a[p, g]) >= 10]
            a[p, g + 8] = far[np.random.randint(len(far))]
    return np.exp2(a.ravel()).repeat(32)


def f64(x):
    return np.asarray(x).astype(np.float64)


def striped8(idx):
    return np.concatenate([v.reshape(-1, 16).T for v in idx]).astype(np.uint16)


def unstriped8(offs):
    return np.stack([offs[16 * g:16 * g + 16].T.reshape(-1) for g in range(8)]).astype(np.int64)


E2M1 = np.array([0.0, 0.5, 1.0, 1.5, 2.0, 3.0, 4.0, 6.0, -0.0, -0.5, -1.0, -1.5, -2.0, -3.0, -4.0, -6.0])


def pack_weight(w, fmt):
    k, n = w.shape
    w = f64(np.asarray(w, np.float32).astype(ml_dtypes.bfloat16)).reshape(k // 32, 32, n)
    amax = np.abs(w).max(1)
    if fmt == "e4m3":
        byte = np.frexp(amax)[1] - 1 + 127 - 7
    else:
        mant, ex = np.frexp(amax / 6.0)
        byte = np.where(mant > 0.5, ex, ex - 1) + 127
    byte = np.clip(np.where(amax > 0, byte, 1), 1, 254)
    scaled = (w * np.exp2(127.0 - byte)[:, None, :]).reshape(k, n).astype(np.float32)
    by_word = np.ascontiguousarray(scaled.reshape(k // 512, 128, 4, n).transpose(0, 1, 3, 2))
    if fmt == "e4m3":
        words = by_word.astype(ml_dtypes.float8_e4m3fn).view(np.uint8)
    else:
        c = by_word.astype(ml_dtypes.float4_e2m1fn).view(np.uint8) & 0xF
        words = (c[..., 0::2] | (c[..., 1::2] << 4)).reshape(k // 512, 128, 2 * n)
    return np.ascontiguousarray(words), np.ascontiguousarray(byte.astype(np.uint8).reshape(k // 512, 16, n))


def unpack_weight(words, scales, fmt):
    g, _, n = scales.shape
    words = np.ascontiguousarray(words).reshape(g, 128, n, -1)
    if fmt == "e4m3":
        vals = words.view(ml_dtypes.float8_e4m3fn).astype(np.float64)
    else:
        nib = np.empty((g, 128, n, 4), np.uint8)
        nib[..., 0::2] = words & 0xF
        nib[..., 1::2] = words >> 4
        vals = E2M1[nib]
    vals = vals * np.repeat(np.exp2(scales.astype(np.float64) - 127.0), 8, axis=1)[..., None]
    return vals.transpose(0, 1, 3, 2).reshape(g * 512, n)


def gelu(f):
    return 0.5 * f * (1.0 + np.tanh(np.sqrt(2.0 / np.pi) * (f + 0.044715 * f**3)))


K, L, N, T, J = 512, 512, 512, 2048, 1024


def setup_inputs():
    n = np.random.standard_normal
    s = mx_kscale(K)[:, None]
    s2 = mx_kscale(L)[:, None]
    p_wa = pack_weight(n((K, N)) / np.sqrt(K) / s, "e2m1")
    return {
        "xT": (n((K, T)) * s).astype(np.float32),
        "wgt": np.repeat(np.random.uniform(0.5, 2.0, (8, J)), 16, axis=0).astype(np.float32),
        "zT": (n((L, T)) * s2).astype(np.float32),
        "wgt2": np.repeat(np.random.uniform(0.5, 2.0, (8, J)), 16, axis=0).astype(np.float32),
        "wa_words": p_wa[0],
        "wa_scales": p_wa[1],
        "wb": (n((L, N)) / np.sqrt(L) / s2).astype(np.float32),
        "b": (0.3 * n(N)).astype(np.float32),
        "offs": striped8(np.stack([np.random.permutation(T)[:J] for _ in range(8)])),
        "offs2": striped8(np.stack([np.random.permutation(T)[:J] for _ in range(8)])),
    }


def reference(xT, wgt, zT, wgt2, wa_words, wa_scales, wb, b, offs, offs2):
    idx = unstriped8(offs)
    idx2 = unstriped8(offs2)
    rows = np.arange(K)
    xg = f64(wgt)[rows // 4 % 128] * f64(xT)[rows[:, None], idx[rows % 512 // 64]]
    xT_ = mxq(xg, 0, "e4m3")
    rows = np.arange(L)
    xg = f64(wgt2)[rows // 4 % 128] * f64(zT)[rows[:, None], idx2[rows % 512 // 64]]
    zT_ = mxq(xg, 0, "e4m3")
    wa_ = unpack_weight(wa_words, wa_scales, "e2m1")
    wb_ = mxq(f64(wb), 0, "e4m3")
    ya = wa_.T @ xT_
    yb = wb_.T @ zT_
    return gelu(np.abs(ya - yb) + f64(b)[:, None])

@@ -1,0 +1,245 @@
+from contextlib import ExitStack
+
+import concourse.mybir as mybir
+from concourse.masks import make_identity
+
+K, N, T, J = 512, 512, 2048, 1024
+FLOPS = 2 * 2 * K * N * J
+BYTES = 4 * (2 * K * T + 2 * 8 * J + K * N + N + N * J) + K * N // 2 + 16 * N + 2 * 2 * 8 * J
+
+F32 = mybir.dt.float32
+BF16 = mybir.dt.bfloat16
+I32 = mybir.dt.int32
+U32 = mybir.dt.uint32
+U16 = mybir.dt.uint16
+U8 = mybir.dt.uint8
+FP8X4 = mybir.dt.float8_e4m3fn_x4
+FP4X4 = mybir.dt.float4_e2m1fn_x4
+ALU = mybir.AluOpType
+ACT = mybir.ActivationFunctionType
+
+P = 128
+PACK = 4
+HEADS = 8
+GROUP = 16
+BANK = 512
+HALF = 512
+CHUNK = 256
+CHUNKS = J // CHUNK
+
+
+def woven(src):
+    return src.rearrange("p t (c i) -> p c t i", i=4)
+
+
+def woven_out(dst):
+    return dst.rearrange("p (c i) t -> p c t i", i=4)
+
+
+def tile_list_absd_gelu_kernel(
+    tc, xT, wgt, zT, wgt2, wa_words, wa_scales, wb, b, offs, offs2, out
+):
+    nc = tc.nc
+    with ExitStack() as ctx:
+        keep = ctx.enter_context(tc.tile_pool(name="keep", bufs=1))
+        psum = ctx.enter_context(tc.psum_pool(name="psum", bufs=1))
+
+        def bank(i, shape, name):
+            return psum.tile(shape, F32, name=name, tag="bank%d" % i)
+
+        x_list = keep.tile([P, J // 16], U16, name="x_list")
+        z_list = keep.tile([P, J // 16], U16, name="z_list")
+        head_rows = keep.tile([P, P], F32, name="head_rows")
+        x_planes = [keep.tile([P, T], F32, name="x_plane%d" % t) for t in range(PACK)]
+        z_planes = [keep.tile([P, T], F32, name="z_plane%d" % t) for t in range(PACK)]
+        wa_codes = keep.tile([P, 2 * N], U8, name="wa_codes", align_bytes=64)
+        wa_plane = keep.tile([P, N], U8, name="wa_plane", align_bytes=64)
+        wb_raw = keep.tile([P, PACK, N], F32, name="wb_raw")
+        bias = keep.tile([P, N // P], F32, name="bias")
+        ident = keep.tile([P, P], F32, name="ident")
+        warm_in = keep.tile([P, 8], F32, name="warm_in")
+        warm_out = keep.tile([P, 8], F32, name="warm_out")
+
+        nc.vector.memset(warm_in[:], 0.0)
+        nc.scalar.activation(warm_out[:], warm_in[:], ACT.Gelu_apprx_tanh)
+        make_identity(nc, ident[:])
+        nc.vector.memset(wa_plane[:].bitcast(I32), 0)
+
+        xT_planes = xT.rearrange("(p t) n -> t p n", t=PACK)
+        zT_planes = zT.rearrange("(p t) n -> t p n", t=PACK)
+        for s, w in enumerate((wgt, wgt2)):
+            nc.sync.dma_start(
+                out=head_rows[64 * s : 64 * (s + 1), :],
+                in_=w.rearrange("(h r) (c j) -> r h c j", r=GROUP, j=P)[0],
+            )
+        nc.sync.dma_start(x_list[:], offs)
+        nc.sync.dma_start(out=x_planes[0][:], in_=xT_planes[0])
+        nc.sync.dma_start(out=x_planes[1][:], in_=xT_planes[1])
+        nc.sync.dma_start(z_list[:], offs2)
+        nc.sync.dma_start(out=x_planes[2][:], in_=xT_planes[2])
+        nc.sync.dma_start(out=x_planes[3][:], in_=xT_planes[3])
+        nc.sync.dma_start(out=wa_codes[:].bitcast(I32), in_=wa_words[0].bitcast(I32))
+        with nc.allow_non_contiguous_dma(reason="one bias value a partition and output tile"):
+            nc.sync.dma_start(out=bias[:], in_=b.rearrange("(c p) -> p c", p=P))
+        for t in range(PACK):
+            if t == 2:
+                nc.sync.dma_start(out=wb_raw[:], in_=wb.rearrange("(p t) n -> p t n", t=PACK))
+            nc.sync.dma_start(out=z_planes[t][:], in_=zT_planes[t])
+        for q in range(4):
+            nc.gpsimd.dma_start(
+                out=wa_plane[32 * q : 32 * q + 4, :].bitcast(I32),
+                in_=wa_scales[0, 4 * q : 4 * q + 4, :].bitcast(I32),
+            )
+
+        turned = bank(0, [P, P], "turned")
+        nc.tensor.transpose(turned[:], head_rows[:], ident[:])
+        x_weights = keep.tile([P, J], F32, name="x_weights")
+        zg = [keep.tile([P, PACK, HALF], F32, name="zg%d" % u) for u in range(2)]
+        z_weights_late = keep.tile([P, HALF], F32, name="z_weights_late")
+        z_weights = [zg[1][:, 2, :], z_weights_late[:]]
+        weights = [[x_weights[:, :HALF], x_weights[:, HALF:]], z_weights]
+        by_head = turned[:].rearrange("j (s h c) -> j s c h", s=2, h=HEADS)
+        for s in range(2):
+            for u in range(2):
+                copy = nc.vector.tensor_copy if (s, u) == (0, 0) else nc.scalar.copy
+                spread = keep.tile([P, 4, HEADS, GROUP], F32, name="spread%d%d" % (s, u))
+                copy(
+                    out=spread[:],
+                    in_=by_head[:, s, 4 * u : 4 * u + 4, :].unsqueeze(3).to_broadcast([P, 4, HEADS, GROUP]),
+                )
+                back = bank(1 + 2 * s + u, [P, 4, P], "back%d%d" % (s, u))
+                for c in range(4):
+                    nc.tensor.transpose(back[:, c, :], spread[:, c].rearrange("j h r -> j (h r)"), ident[:])
+                copy(out=weights[s][u], in_=back[:].rearrange("p c j -> p (c j)"))
+
+        def gather_x(t, lo, hi):
+            nc.vector.tensor_tensor(
+                xg[:, t, lo:hi], x_planes[t][:].indirect(x_list[:, lo // 16 : hi // 16]), x_weights[:, lo:hi], ALU.mult
+            )
+
+        def gather_z(t, lo, hi):
+            u = lo // HALF
+            cols = slice(lo - u * HALF, hi - u * HALF)
+            nc.vector.tensor_tensor(
+                zg[u][:, t, cols],
+                z_planes[t][:].indirect(z_list[:, lo // 16 : hi // 16]),
+                z_weights[u][:, cols],
+                ALU.mult,
+            )
+
+        def quantize(name, grouped, width):
+            codes = keep.tile([P, width], U32, name=name + "_codes", align_bytes=64)
+            plane = keep.tile([P, width], U8, name=name + "_plane", align_bytes=64)
+            nc.vector.quantize_mx(
+                out=codes[:].bitcast(FP8X4), scales=plane[:], in_=grouped[:].rearrange("p c t -> p (c t)")
+            )
+            return codes, plane
+
+        xg = keep.tile([P, PACK, J], F32, name="xg")
+        for t in range(PACK):
+            cuts = (0, HALF, J) if t in (0, 3) else (0, J)
+            for lo, hi in zip(cuts, cuts[1:]):
+                gather_x(t, lo, hi)
+        x_grouped = []
+        for u in range(2):
+            grouped = keep.tile([P, HALF, PACK], BF16, name="x_grouped%d" % u, align_bytes=64)
+            nc.scalar.copy(out=woven_out(grouped[:]), in_=woven(xg[:, :, HALF * u : HALF * (u + 1)]))
+            x_grouped.append(grouped)
+
+        gather_z(0, 0, HALF)
+        gather_z(0, HALF, J)
+
+        wb_grouped = keep.tile([P, N, PACK], BF16, name="wb_grouped", align_bytes=64)
+        nc.scalar.activation(woven_out(wb_grouped[:]), woven(wb_raw[:]), ACT.Copy, scale=-1.0)
+
+        x_q = [quantize("x%d" % u, x_grouped[u], HALF) for u in range(2)]
+        sums = {}
+        for c in range(CHUNKS):
+            codes, plane = x_q[c * CHUNK // HALF]
+            for pair in range(2):
+                acc = bank(2 * c + pair, [P, 2, CHUNK], "sum%d%d" % (c, pair))
+                sums[c, pair] = acc
+                for m in range(2):
+                    nt = 2 * pair + m
+                    for v in range(CHUNK // P):
+                        col = c * CHUNK % HALF + v * P
+                        nc.tensor.matmul_mx(
+                            out=acc[:, m, v * P : (v + 1) * P],
+                            lhsT=wa_codes[:, 2 * P * nt : 2 * P * (nt + 1)].bitcast(FP4X4),
+                            lhsT_scale=wa_plane[:, P * nt : P * (nt + 1)],
+                            rhs=codes[:, col : col + P].bitcast(FP8X4),
+                            rhs_scale=plane[:, col : col + P],
+                            start=(m == 0 and v == 0),
+                            stop=False,
+                        )
+
+        gather_z(1, 0, HALF)
+        gather_z(1, HALF, J)
+        gather_z(2, 0, HALF)
+        wb_codes, wb_plane = quantize("wb", wb_grouped, N)
+
+        out_tiles = out.rearrange("(nt p) j -> p nt j", p=P)
+        z_grouped = {}
+
+        def last_gather(c):
+            gather_z(3, c * CHUNK, (c + 1) * CHUNK)
+
+        def weave(c):
+            grouped = keep.tile([P, CHUNK, PACK], BF16, name="z_grouped%d" % c, align_bytes=64)
+            copy = nc.scalar.copy if c < 2 else nc.vector.tensor_copy
+            col = c * CHUNK % HALF
+            copy(out=woven_out(grouped[:]), in_=woven(zg[c * CHUNK // HALF][:, :, col : col + CHUNK]))
+            z_grouped[c] = grouped
+
+        def finish(c):
+            codes, plane = quantize("z%d" % c, z_grouped[c], CHUNK)
+            mags = []
+            for pair in range(2):
+                acc = sums[c, pair]
+                for m in range(2):
+                    nt = 2 * pair + m
+                    nc.tensor.matmul_mx(
+                        out=acc[:, m, :],
+                        lhsT=wb_codes[:, P * nt : P * (nt + 1)].bitcast(FP8X4),
+                        lhsT_scale=wb_plane[:, P * nt : P * (nt + 1)],
+                        rhs=codes[:].bitcast(FP8X4),
+                        rhs_scale=plane[:],
+                        start=False,
+                        stop=(m == 1),
+                    )
+                mag = keep.tile([P, 2 * CHUNK], F32, name="mag%d%d" % (c, pair))
+                flat = acc[:].rearrange("p m j -> p (m j)")
+                if c == CHUNKS - 1:
+                    neg = keep.tile([P, 2 * CHUNK], F32, name="neg%d" % pair)
+                    nc.vector.tensor_scalar(neg[:], flat, -1.0, None, ALU.mult)
+                    nc.vector.tensor_tensor(mag[:], neg[:], flat, ALU.max)
+                else:
+                    nc.scalar.activation(mag[:], flat, ACT.Abs)
+                mags.append(mag)
+            for pair in range(2):
+                res = keep.tile([P, 2, CHUNK], F32, name="res%d%d" % (c, pair))
+                for m in range(2):
+                    nt = 2 * pair + m
+                    nc.scalar.activation(
+                        res[:, m, :],
+                        mags[pair][:, m * CHUNK : (m + 1) * CHUNK],
+                        ACT.Gelu_apprx_tanh,
+                        bias=bias[:, nt : nt + 1],
+                    )
+                nc.sync.dma_start(
+                    out=out_tiles[:, 2 * pair : 2 * pair + 2, c * CHUNK : (c + 1) * CHUNK], in_=res[:]
+                )
+
+        last_gather(0)
+        weave(0)
+        last_gather(1)
+        weave(1)
+        gather_z(2, HALF, J)
+        finish(0)
+        last_gather(2)
+        finish(1)
+        last_gather(3)
+        weave(2)
+        weave(3)
+        finish(2)
+        finish(3)

@@ -94,23 +94,43 @@ def tile_list_absd_gelu_kernel(
         turned = bank(0, [P, P], "turned")
         nc.tensor.transpose(turned[:], head_rows[:], ident[:])
         x_weights = keep.tile([P, J], F32, name="x_weights")
-        zg = [keep.tile([P, PACK, HALF], F32, name="zg%d" % u) for u in range(2)]
+        zg_early = keep.tile([P, PACK, HALF], F32, name="zg_early")
+        pitch = 640
+        late2 = keep.tile([P, PACK * pitch], F32, name="late2", align_bytes=64)
+        late3 = keep.tile([P, PACK * CHUNK], F32, name="late3", align_bytes=64)
+        zg = [
+            zg_early[:, :, :CHUNK],
+            zg_early[:, :, CHUNK:],
+            late2[:].rearrange("p (t w) -> p t w", t=PACK)[:, :, :CHUNK],
+            late3[:].rearrange("p (t w) -> p t w", t=PACK),
+        ]
         z_weights_late = keep.tile([P, HALF], F32, name="z_weights_late")
-        z_weights = [zg[1][:, 2, :], z_weights_late[:]]
-        weights = [[x_weights[:, :HALF], x_weights[:, HALF:]], z_weights]
+        lap = 128
+        z_weights = [late2[:, CHUNK : CHUNK + HALF], z_weights_late[:]]
+        z_grouped = [
+            late2[:, 3 * pitch + 64 - HALF : 3 * pitch + 64],
+            late3[:, CHUNK + lap : CHUNK + lap + HALF],
+            keep.tile([P, HALF], F32, name="z_grouped2", align_bytes=64)[:],
+            keep.tile([P, HALF], F32, name="z_grouped3", align_bytes=64)[:],
+        ]
+        z_grouped = [g.bitcast(BF16).rearrange("p (c t) -> p c t", t=PACK) for g in z_grouped]
         by_head = turned[:].rearrange("j (s h c) -> j s c h", s=2, h=HEADS)
-        for s in range(2):
-            for u in range(2):
-                copy = nc.vector.tensor_copy if (s, u) == (0, 0) else nc.scalar.copy
-                spread = keep.tile([P, 4, HEADS, GROUP], F32, name="spread%d%d" % (s, u))
-                copy(
-                    out=spread[:],
-                    in_=by_head[:, s, 4 * u : 4 * u + 4, :].unsqueeze(3).to_broadcast([P, 4, HEADS, GROUP]),
-                )
-                back = bank(1 + 2 * s + u, [P, 4, P], "back%d%d" % (s, u))
-                for c in range(4):
-                    nc.tensor.transpose(back[:, c, :], spread[:, c].rearrange("j h r -> j (h r)"), ident[:])
-                copy(out=weights[s][u], in_=back[:].rearrange("p c j -> p (c j)"))
+        pieces = [
+            (0, 0, 2, x_weights[:, :CHUNK]),
+            (0, 2, 4, x_weights[:, CHUNK:HALF]),
+            (0, 4, 8, x_weights[:, HALF:]),
+            (1, 0, 4, z_weights[0]),
+            (1, 4, 8, z_weights[1]),
+        ]
+        for i, (s, c0, c1, dst) in enumerate(pieces):
+            copy = nc.vector.tensor_copy if i == 0 else nc.scalar.copy
+            count = c1 - c0
+            spread = keep.tile([P, count, HEADS, GROUP], F32, name="spread%d" % i)
+            copy(out=spread[:], in_=by_head[:, s, c0:c1, :].unsqueeze(3).to_broadcast([P, count, HEADS, GROUP]))
+            back = bank(1 + i, [P, count, P], "back%d" % i)
+            for c in range(count):
+                nc.tensor.transpose(back[:, c, :], spread[:, c].rearrange("j h r -> j (h r)"), ident[:])
+            copy(out=dst, in_=back[:].rearrange("p c j -> p (c j)"))
 
         def gather_x(t, lo, hi):
             nc.vector.tensor_tensor(
@@ -121,7 +141,7 @@ def tile_list_absd_gelu_kernel(
             u = lo // HALF
             cols = slice(lo - u * HALF, hi - u * HALF)
             nc.vector.tensor_tensor(
-                zg[u][:, t, cols],
+                zg_early[:, t, cols] if u == 0 else zg[lo // CHUNK][:, t, :],
                 z_planes[t][:].indirect(z_list[:, lo // 16 : hi // 16]),
                 z_weights[u][:, cols],
                 ALU.mult,
@@ -131,13 +151,13 @@ def tile_list_absd_gelu_kernel(
             codes = keep.tile([P, width], U32, name=name + "_codes", align_bytes=64)
             plane = keep.tile([P, width], U8, name=name + "_plane", align_bytes=64)
             nc.vector.quantize_mx(
-                out=codes[:].bitcast(FP8X4), scales=plane[:], in_=grouped[:].rearrange("p c t -> p (c t)")
+                out=codes[:].bitcast(FP8X4), scales=plane[:], in_=grouped.rearrange("p c t -> p (c t)")
             )
             return codes, plane
 
         xg = keep.tile([P, PACK, J], F32, name="xg")
         for t in range(PACK):
-            cuts = (0, HALF, J) if t in (0, 3) else (0, J)
+            cuts = ((0, CHUNK, HALF, J), (0, J), (0, J), (0, HALF, J))[t]
             for lo, hi in zip(cuts, cuts[1:]):
                 gather_x(t, lo, hi)
         x_grouped = []
@@ -147,12 +167,13 @@ def tile_list_absd_gelu_kernel(
             x_grouped.append(grouped)
 
         gather_z(0, 0, HALF)
-        gather_z(0, HALF, J)
+        gather_z(0, HALF, HALF + CHUNK)
+        gather_z(0, HALF + CHUNK, J)
 
         wb_grouped = keep.tile([P, N, PACK], BF16, name="wb_grouped", align_bytes=64)
         nc.scalar.activation(woven_out(wb_grouped[:]), woven(wb_raw[:]), ACT.Copy, scale=-1.0)
 
-        x_q = [quantize("x%d" % u, x_grouped[u], HALF) for u in range(2)]
+        x_q = [quantize("x%d" % u, x_grouped[u][:], HALF) for u in range(2)]
         sums = {}
         for c in range(CHUNKS):
             codes, plane = x_q[c * CHUNK // HALF]
@@ -174,22 +195,17 @@ def tile_list_absd_gelu_kernel(
                         )
 
         gather_z(1, 0, HALF)
-        gather_z(1, HALF, J)
         gather_z(2, 0, HALF)
-        wb_codes, wb_plane = quantize("wb", wb_grouped, N)
+        wb_codes, wb_plane = quantize("wb", wb_grouped[:], N)
 
         out_tiles = out.rearrange("(nt p) j -> p nt j", p=P)
-        z_grouped = {}
 
-        def last_gather(c):
-            gather_z(3, c * CHUNK, (c + 1) * CHUNK)
+        def gather_chunk(t, c):
+            gather_z(t, c * CHUNK, (c + 1) * CHUNK)
 
         def weave(c):
-            grouped = keep.tile([P, CHUNK, PACK], BF16, name="z_grouped%d" % c, align_bytes=64)
             copy = nc.scalar.copy if c < 2 else nc.vector.tensor_copy
-            col = c * CHUNK % HALF
-            copy(out=woven_out(grouped[:]), in_=woven(zg[c * CHUNK // HALF][:, :, col : col + CHUNK]))
-            z_grouped[c] = grouped
+            copy(out=woven_out(z_grouped[c]), in_=woven(zg[c]))
 
         def finish(c):
             codes, plane = quantize("z%d" % c, z_grouped[c], CHUNK)
@@ -209,14 +225,14 @@ def tile_list_absd_gelu_kernel(
                     )
                 mag = keep.tile([P, 2 * CHUNK], F32, name="mag%d%d" % (c, pair))
                 flat = acc[:].rearrange("p m j -> p (m j)")
-                if c == CHUNKS - 1:
+                if (c, pair) == (CHUNKS - 1, 0):
                     neg = keep.tile([P, 2 * CHUNK], F32, name="neg%d" % pair)
                     nc.vector.tensor_scalar(neg[:], flat, -1.0, None, ALU.mult)
                     nc.vector.tensor_tensor(mag[:], neg[:], flat, ALU.max)
                 else:
                     nc.scalar.activation(mag[:], flat, ACT.Abs)
                 mags.append(mag)
-            for pair in range(2):
+            for pair in (1, 0) if c == CHUNKS - 1 else (0, 1):
                 res = keep.tile([P, 2, CHUNK], F32, name="res%d%d" % (c, pair))
                 for m in range(2):
                     nt = 2 * pair + m
@@ -226,20 +242,26 @@ def tile_list_absd_gelu_kernel(
                         ACT.Gelu_apprx_tanh,
                         bias=bias[:, nt : nt + 1],
                     )
-                nc.sync.dma_start(
-                    out=out_tiles[:, 2 * pair : 2 * pair + 2, c * CHUNK : (c + 1) * CHUNK], in_=res[:]
-                )
+                    if (c, pair) == (CHUNKS - 1, 0):
+                        nc.sync.dma_start(out=out_tiles[:, nt, c * CHUNK : (c + 1) * CHUNK], in_=res[:, m, :])
+                if (c, pair) != (CHUNKS - 1, 0):
+                    nc.sync.dma_start(
+                        out=out_tiles[:, 2 * pair : 2 * pair + 2, c * CHUNK : (c + 1) * CHUNK], in_=res[:]
+                    )
 
-        last_gather(0)
+        gather_chunk(3, 0)
         weave(0)
-        last_gather(1)
+        gather_chunk(3, 1)
         weave(1)
-        gather_z(2, HALF, J)
+        gather_chunk(1, 2)
         finish(0)
-        last_gather(2)
+        gather_chunk(2, 2)
+        gather_chunk(3, 2)
         finish(1)
-        last_gather(3)
         weave(2)
-        weave(3)
+        gather_chunk(1, 3)
         finish(2)
+        gather_chunk(2, 3)
+        gather_chunk(3, 3)
+        weave(3)
         finish(3)

@@ -118,19 +118,20 @@ def tile_list_absd_gelu_kernel(
         pieces = [
             (0, 0, 2, x_weights[:, :CHUNK]),
             (0, 2, 4, x_weights[:, CHUNK:HALF]),
-            (0, 4, 8, x_weights[:, HALF:]),
+            (0, 4, 6, x_weights[:, HALF : HALF + CHUNK]),
+            (0, 6, 8, x_weights[:, HALF + CHUNK :]),
             (1, 0, 4, z_weights[0]),
             (1, 4, 8, z_weights[1]),
         ]
         for i, (s, c0, c1, dst) in enumerate(pieces):
-            copy = nc.vector.tensor_copy if i == 0 else nc.scalar.copy
+            copy = nc.vector.tensor_copy if s == 0 else nc.scalar.copy
             count = c1 - c0
-            spread = keep.tile([P, count, HEADS, GROUP], F32, name="spread%d" % i)
+            spread = keep.tile([P, count, HEADS, GROUP], F32, name="spread%d" % i, tag="spread%d" % min(i, 3))
             copy(out=spread[:], in_=by_head[:, s, c0:c1, :].unsqueeze(3).to_broadcast([P, count, HEADS, GROUP]))
             back = bank(1 + i, [P, count, P], "back%d" % i)
             for c in range(count):
                 nc.tensor.transpose(back[:, c, :], spread[:, c].rearrange("j h r -> j (h r)"), ident[:])
-            copy(out=dst, in_=back[:].rearrange("p c j -> p (c j)"))
+            nc.scalar.copy(out=dst, in_=back[:].rearrange("p c j -> p (c j)"))
 
         def gather_x(t, lo, hi):
             nc.vector.tensor_tensor(
@@ -157,7 +158,7 @@ def tile_list_absd_gelu_kernel(
 
         xg = keep.tile([P, PACK, J], F32, name="xg")
         for t in range(PACK):
-            cuts = ((0, CHUNK, HALF, J), (0, J), (0, J), (0, HALF, J))[t]
+            cuts = ((0, CHUNK, HALF, HALF + CHUNK, J), (0, J), (0, J), (0, HALF, J))[t]
             for lo, hi in zip(cuts, cuts[1:]):
                 gather_x(t, lo, hi)
         x_grouped = []

@@ -70,7 +70,7 @@ def tile_list_absd_gelu_kernel(
         for s, w in enumerate((wgt, wgt2)):
             nc.sync.dma_start(
                 out=head_rows[64 * s : 64 * (s + 1), :],
-                in_=w.rearrange("(h r) (c j) -> r h c j", r=GROUP, j=P)[0],
+                in_=w.rearrange("p (a c j) -> (p a) c j", a=2, j=P)[0 : 2 * P : GROUP + 1],
             )
         nc.sync.dma_start(x_list[:], offs)
         nc.sync.dma_start(out=x_planes[0][:], in_=xT_planes[0])
@@ -114,6 +114,7 @@ def tile_list_absd_gelu_kernel(
             keep.tile([P, HALF], F32, name="z_grouped3", align_bytes=64)[:],
         ]
         z_grouped = [g.bitcast(BF16).rearrange("p (c t) -> p c t", t=PACK) for g in z_grouped]
+        first_weights = keep.tile([P, CHUNK], F32, name="first_weights", tag="x1_codes", align_bytes=64)
         by_head = turned[:].rearrange("j (s h c) -> j s c h", s=2, h=HEADS)
         pieces = [
             (0, 0, 2, x_weights[:, :CHUNK]),
@@ -132,6 +133,8 @@ def tile_list_absd_gelu_kernel(
             for c in range(count):
                 nc.tensor.transpose(back[:, c, :], spread[:, c].rearrange("j h r -> j (h r)"), ident[:])
             nc.scalar.copy(out=dst, in_=back[:].rearrange("p c j -> p (c j)"))
+            if (s, c0) == (1, 0):
+                nc.scalar.copy(out=first_weights[:], in_=back[:, :2, :].rearrange("p c j -> p (c j)"))
 
         def gather_x(t, lo, hi):
             nc.vector.tensor_tensor(
@@ -144,12 +147,12 @@ def tile_list_absd_gelu_kernel(
             nc.vector.tensor_tensor(
                 zg_early[:, t, cols] if u == 0 else zg[lo // CHUNK][:, t, :],
                 z_planes[t][:].indirect(z_list[:, lo // 16 : hi // 16]),
-                z_weights[u][:, cols],
+                first_weights[:] if (t, lo) == (PACK - 1, 0) else z_weights[u][:, cols],
                 ALU.mult,
             )
 
         def quantize(name, grouped, width):
-            codes = keep.tile([P, width], U32, name=name + "_codes", align_bytes=64)
+            codes = keep.tile([P, width], U32, name=name + "_codes", tag=name + "_codes", align_bytes=64)
             plane = keep.tile([P, width], U8, name=name + "_plane", align_bytes=64)
             nc.vector.quantize_mx(
                 out=codes[:].bitcast(FP8X4), scales=plane[:], in_=grouped.rearrange("p c t -> p (c t)")
@@ -174,12 +177,13 @@ def tile_list_absd_gelu_kernel(
         wb_grouped = keep.tile([P, N, PACK], BF16, name="wb_grouped", align_bytes=64)
         nc.scalar.activation(woven_out(wb_grouped[:]), woven(wb_raw[:]), ACT.Copy, scale=-1.0)
 
-        x_q = [quantize("x%d" % u, x_grouped[u][:], HALF) for u in range(2)]
+        x_q = [quantize("x0", x_grouped[0][:], HALF)]
         sums = {}
-        for c in range(CHUNKS):
+
+        def open_sums(c):
             codes, plane = x_q[c * CHUNK // HALF]
             for pair in range(2):
-                acc = bank(2 * c + pair, [P, 2, CHUNK], "sum%d%d" % (c, pair))
+                acc = bank(2 * (c % 2) + pair, [P, 2, CHUNK], "sum%d%d" % (c, pair))
                 sums[c, pair] = acc
                 for m in range(2):
                     nt = 2 * pair + m
@@ -195,6 +199,8 @@ def tile_list_absd_gelu_kernel(
                             stop=False,
                         )
 
+        open_sums(0)
+        open_sums(1)
         gather_z(1, 0, HALF)
         gather_z(2, 0, HALF)
         wb_codes, wb_plane = quantize("wb", wb_grouped[:], N)
@@ -255,10 +261,13 @@ def tile_list_absd_gelu_kernel(
         gather_chunk(3, 1)
         weave(1)
         gather_chunk(1, 2)
+        x_q.append(quantize("x1", x_grouped[1][:], HALF))
         finish(0)
+        open_sums(2)
         gather_chunk(2, 2)
         gather_chunk(3, 2)
         finish(1)
+        open_sums(3)
         weave(2)
         gather_chunk(1, 3)
         finish(2)

@@ -56,6 +56,7 @@ def tile_list_absd_gelu_kernel(
         wa_plane = keep.tile([P, N], U8, name="wa_plane", align_bytes=64)
         wb_raw = keep.tile([P, PACK, N], F32, name="wb_raw")
         bias = keep.tile([P, N // P], F32, name="bias")
+        bias_rows = keep.tile([P, P], F32, name="bias_rows")
         ident = keep.tile([P, P], F32, name="ident")
         warm_in = keep.tile([P, 8], F32, name="warm_in")
         warm_out = keep.tile([P, 8], F32, name="warm_out")
@@ -64,6 +65,7 @@ def tile_list_absd_gelu_kernel(
         nc.scalar.activation(warm_out[:], warm_in[:], ACT.Gelu_apprx_tanh)
         make_identity(nc, ident[:])
         nc.vector.memset(wa_plane[:].bitcast(I32), 0)
+        nc.vector.memset(bias_rows[:], 0.0)
 
         xT_planes = xT.rearrange("(p t) n -> t p n", t=PACK)
         zT_planes = zT.rearrange("(p t) n -> t p n", t=PACK)
@@ -78,13 +80,12 @@ def tile_list_absd_gelu_kernel(
         nc.sync.dma_start(z_list[:], offs2)
         nc.sync.dma_start(out=x_planes[2][:], in_=xT_planes[2])
         nc.sync.dma_start(out=x_planes[3][:], in_=xT_planes[3])
-        nc.sync.dma_start(out=wa_codes[:].bitcast(I32), in_=wa_words[0].bitcast(I32))
-        with nc.allow_non_contiguous_dma(reason="one bias value a partition and output tile"):
-            nc.sync.dma_start(out=bias[:], in_=b.rearrange("(c p) -> p c", p=P))
         for t in range(PACK):
             if t == 2:
                 nc.sync.dma_start(out=wb_raw[:], in_=wb.rearrange("(p t) n -> p t n", t=PACK))
             nc.sync.dma_start(out=z_planes[t][:], in_=zT_planes[t])
+        nc.sync.dma_start(out=wa_codes[:].bitcast(I32), in_=wa_words[0].bitcast(I32))
+        nc.sync.dma_start(out=bias_rows[: N // P, :], in_=b.rearrange("(c p) -> c p", p=P))
         for q in range(4):
             nc.gpsimd.dma_start(
                 out=wa_plane[32 * q : 32 * q + 4, :].bitcast(I32),
@@ -262,6 +263,9 @@ def tile_list_absd_gelu_kernel(
         weave(1)
         gather_chunk(1, 2)
         x_q.append(quantize("x1", x_grouped[1][:], HALF))
+        bias_turned = bank(7, [P, P], "bias_turned")
+        nc.tensor.transpose(bias_turned[:], bias_rows[:], ident[:])
+        nc.scalar.copy(out=bias[:], in_=bias_turned[:, : N // P])
         finish(0)
         open_sums(2)
         gather_chunk(2, 2)

@@ -115,7 +115,6 @@ def tile_list_absd_gelu_kernel(
             keep.tile([P, HALF], F32, name="z_grouped3", align_bytes=64)[:],
         ]
         z_grouped = [g.bitcast(BF16).rearrange("p (c t) -> p c t", t=PACK) for g in z_grouped]
-        first_weights = keep.tile([P, CHUNK], F32, name="first_weights", tag="x1_codes", align_bytes=64)
         by_head = turned[:].rearrange("j (s h c) -> j s c h", s=2, h=HEADS)
         pieces = [
             (0, 0, 2, x_weights[:, :CHUNK]),
@@ -134,8 +133,6 @@ def tile_list_absd_gelu_kernel(
             for c in range(count):
                 nc.tensor.transpose(back[:, c, :], spread[:, c].rearrange("j h r -> j (h r)"), ident[:])
             nc.scalar.copy(out=dst, in_=back[:].rearrange("p c j -> p (c j)"))
-            if (s, c0) == (1, 0):
-                nc.scalar.copy(out=first_weights[:], in_=back[:, :2, :].rearrange("p c j -> p (c j)"))
 
         def gather_x(t, lo, hi):
             nc.vector.tensor_tensor(
@@ -146,14 +143,14 @@ def tile_list_absd_gelu_kernel(
             u = lo // HALF
             cols = slice(lo - u * HALF, hi - u * HALF)
             nc.vector.tensor_tensor(
-                zg_early[:, t, cols] if u == 0 else zg[lo // CHUNK][:, t, :],
+                zg_early[:, t, cols] if u == 0 else zg[lo // CHUNK][:, t, lo % CHUNK : lo % CHUNK + hi - lo],
                 z_planes[t][:].indirect(z_list[:, lo // 16 : hi // 16]),
-                first_weights[:] if (t, lo) == (PACK - 1, 0) else z_weights[u][:, cols],
+                z_weights[u][:, cols],
                 ALU.mult,
             )
 
         def quantize(name, grouped, width):
-            codes = keep.tile([P, width], U32, name=name + "_codes", tag=name + "_codes", align_bytes=64)
+            codes = keep.tile([P, width], U32, name=name + "_codes", align_bytes=64)
             plane = keep.tile([P, width], U8, name=name + "_plane", align_bytes=64)
             nc.vector.quantize_mx(
                 out=codes[:].bitcast(FP8X4), scales=plane[:], in_=grouped.rearrange("p c t -> p (c t)")
@@ -178,7 +175,7 @@ def tile_list_absd_gelu_kernel(
         wb_grouped = keep.tile([P, N, PACK], BF16, name="wb_grouped", align_bytes=64)
         nc.scalar.activation(woven_out(wb_grouped[:]), woven(wb_raw[:]), ACT.Copy, scale=-1.0)
 
-        x_q = [quantize("x0", x_grouped[0][:], HALF)]
+        x_q = [quantize("x%d" % u, x_grouped[u][:], HALF) for u in range(2)]
         sums = {}
 
         def open_sums(c):
@@ -201,7 +198,6 @@ def tile_list_absd_gelu_kernel(
                         )
 
         open_sums(0)
-        open_sums(1)
         gather_z(1, 0, HALF)
         gather_z(2, 0, HALF)
         wb_codes, wb_plane = quantize("wb", wb_grouped[:], N)
@@ -211,36 +207,48 @@ def tile_list_absd_gelu_kernel(
         def gather_chunk(t, c):
             gather_z(t, c * CHUNK, (c + 1) * CHUNK)
 
+        def parts(c):
+            width = P if c == CHUNKS - 1 else CHUNK
+            return [slice(lo, lo + width) for lo in range(0, CHUNK, width)]
+
         def weave(c):
             copy = nc.scalar.copy if c < 2 else nc.vector.tensor_copy
-            copy(out=woven_out(z_grouped[c]), in_=woven(zg[c]))
+            for cols in parts(c):
+                copy(out=woven_out(z_grouped[c][:, cols, :]), in_=woven(zg[c][:, :, cols]))
 
         def finish(c):
-            codes, plane = quantize("z%d" % c, z_grouped[c], CHUNK)
+            operands = [
+                (cols, quantize("z%d_%d" % (c, cols.start), z_grouped[c][:, cols, :], cols.stop - cols.start))
+                for cols in parts(c)
+            ]
             mags = []
             for pair in range(2):
                 acc = sums[c, pair]
-                for m in range(2):
-                    nt = 2 * pair + m
-                    nc.tensor.matmul_mx(
-                        out=acc[:, m, :],
-                        lhsT=wb_codes[:, P * nt : P * (nt + 1)].bitcast(FP8X4),
-                        lhsT_scale=wb_plane[:, P * nt : P * (nt + 1)],
-                        rhs=codes[:].bitcast(FP8X4),
-                        rhs_scale=plane[:],
-                        start=False,
-                        stop=(m == 1),
-                    )
+                for cols, (codes, plane) in operands:
+                    for m in range(2):
+                        nt = 2 * pair + m
+                        nc.tensor.matmul_mx(
+                            out=acc[:, m, cols],
+                            lhsT=wb_codes[:, P * nt : P * (nt + 1)].bitcast(FP8X4),
+                            lhsT_scale=wb_plane[:, P * nt : P * (nt + 1)],
+                            rhs=codes[:].bitcast(FP8X4),
+                            rhs_scale=plane[:],
+                            start=False,
+                            stop=(m == 1 and cols.stop == CHUNK),
+                        )
                 mag = keep.tile([P, 2 * CHUNK], F32, name="mag%d%d" % (c, pair))
                 flat = acc[:].rearrange("p m j -> p (m j)")
-                if (c, pair) == (CHUNKS - 1, 0):
+                if c == CHUNKS - 1:
                     neg = keep.tile([P, 2 * CHUNK], F32, name="neg%d" % pair)
-                    nc.vector.tensor_scalar(neg[:], flat, -1.0, None, ALU.mult)
-                    nc.vector.tensor_tensor(mag[:], neg[:], flat, ALU.max)
+                    tiles = (slice(0, CHUNK), slice(CHUNK, 2 * CHUNK))
+                    for cols in tiles:
+                        nc.vector.tensor_scalar(neg[:, cols], flat[:, cols], -1.0, None, ALU.mult)
+                    for cols in tiles:
+                        nc.vector.tensor_tensor(mag[:, cols], neg[:, cols], flat[:, cols], ALU.max)
                 else:
                     nc.scalar.activation(mag[:], flat, ACT.Abs)
                 mags.append(mag)
-            for pair in (1, 0) if c == CHUNKS - 1 else (0, 1):
+            for pair in range(2):
                 res = keep.tile([P, 2, CHUNK], F32, name="res%d%d" % (c, pair))
                 for m in range(2):
                     nt = 2 * pair + m
@@ -250,9 +258,9 @@ def tile_list_absd_gelu_kernel(
                         ACT.Gelu_apprx_tanh,
                         bias=bias[:, nt : nt + 1],
                     )
-                    if (c, pair) == (CHUNKS - 1, 0):
+                    if (c, pair) == (CHUNKS - 1, 1):
                         nc.sync.dma_start(out=out_tiles[:, nt, c * CHUNK : (c + 1) * CHUNK], in_=res[:, m, :])
-                if (c, pair) != (CHUNKS - 1, 0):
+                if (c, pair) != (CHUNKS - 1, 1):
                     nc.sync.dma_start(
                         out=out_tiles[:, 2 * pair : 2 * pair + 2, c * CHUNK : (c + 1) * CHUNK], in_=res[:]
                     )
@@ -262,11 +270,11 @@ def tile_list_absd_gelu_kernel(
         gather_chunk(3, 1)
         weave(1)
         gather_chunk(1, 2)
-        x_q.append(quantize("x1", x_grouped[1][:], HALF))
         bias_turned = bank(7, [P, P], "bias_turned")
         nc.tensor.transpose(bias_turned[:], bias_rows[:], ident[:])
         nc.scalar.copy(out=bias[:], in_=bias_turned[:, : N // P])
         finish(0)
+        open_sums(1)
         open_sums(2)
         gather_chunk(2, 2)
         gather_chunk(3, 2)
@@ -276,6 +284,7 @@ def tile_list_absd_gelu_kernel(
         gather_chunk(1, 3)
         finish(2)
         gather_chunk(2, 3)
-        gather_chunk(3, 3)
+        gather_z(3, J - CHUNK, J - P)
+        gather_z(3, J - P, J)
         weave(3)
         finish(3)

@@ -22,10 +22,11 @@ P = 128
 PACK = 4
 HEADS = 8
 GROUP = 16
-BANK = 512
-HALF = 512
-CHUNK = 256
-CHUNKS = J // CHUNK
+TILES = N // P
+PIECE = 256
+CHUNKS = J // PIECE
+EARLY_CHUNKS = 2
+VECTOR_ABS = 3
 
 
 def woven(src):
@@ -36,12 +37,17 @@ def woven_out(dst):
     return dst.rearrange("p (c i) t -> p c t i", i=4)
 
 
+def by_column(pair):
+    return pair.rearrange("p t c -> p c t")
+
+
 def tile_list_absd_gelu_kernel(
     tc, xT, wgt, zT, wgt2, wa_words, wa_scales, wb, b, offs, offs2, out
 ):
     nc = tc.nc
     with ExitStack() as ctx:
         keep = ctx.enter_context(tc.tile_pool(name="keep", bufs=1))
+        over = ctx.enter_context(tc.tile_pool(name="over", bufs=1))
         psum = ctx.enter_context(tc.psum_pool(name="psum", bufs=1))
 
         def bank(i, shape, name):
@@ -49,14 +55,14 @@ def tile_list_absd_gelu_kernel(
 
         x_list = keep.tile([P, J // 16], U16, name="x_list")
         z_list = keep.tile([P, J // 16], U16, name="z_list")
-        head_rows = keep.tile([P, P], F32, name="head_rows")
+        x_rows = keep.tile([P, P], F32, name="x_rows")
+        z_rows = keep.tile([P, P], F32, name="z_rows")
         x_planes = [keep.tile([P, T], F32, name="x_plane%d" % t) for t in range(PACK)]
-        z_planes = [keep.tile([P, T], F32, name="z_plane%d" % t) for t in range(PACK)]
+        z_planes = [keep.tile([P, T], F32, name="z_plane%d" % t, align_bytes=64) for t in range(PACK)]
         wa_codes = keep.tile([P, 2 * N], U8, name="wa_codes", align_bytes=64)
         wa_plane = keep.tile([P, N], U8, name="wa_plane", align_bytes=64)
         wb_raw = keep.tile([P, PACK, N], F32, name="wb_raw")
-        bias = keep.tile([P, N // P], F32, name="bias")
-        bias_rows = keep.tile([P, P], F32, name="bias_rows")
+        bias = keep.tile([P, TILES], F32, name="bias")
         ident = keep.tile([P, P], F32, name="ident")
         warm_in = keep.tile([P, 8], F32, name="warm_in")
         warm_out = keep.tile([P, 8], F32, name="warm_out")
@@ -64,93 +70,70 @@ def tile_list_absd_gelu_kernel(
         nc.vector.memset(warm_in[:], 0.0)
         nc.scalar.activation(warm_out[:], warm_in[:], ACT.Gelu_apprx_tanh)
         make_identity(nc, ident[:])
+        nc.vector.memset(x_rows[64:, :], 0.0)
+        nc.vector.memset(z_rows[64:, :], 0.0)
         nc.vector.memset(wa_plane[:].bitcast(I32), 0)
-        nc.vector.memset(bias_rows[:], 0.0)
 
         xT_planes = xT.rearrange("(p t) n -> t p n", t=PACK)
         zT_planes = zT.rearrange("(p t) n -> t p n", t=PACK)
-        for s, w in enumerate((wgt, wgt2)):
+
+        def load_head_rows(rows, w):
             nc.sync.dma_start(
-                out=head_rows[64 * s : 64 * (s + 1), :],
-                in_=w.rearrange("p (a c j) -> (p a) c j", a=2, j=P)[0 : 2 * P : GROUP + 1],
+                out=rows[:64, :], in_=w.rearrange("p (a c j) -> (p a) c j", a=2, j=P)[0 : 2 * P : GROUP + 1]
             )
+
+        load_head_rows(x_rows, wgt)
         nc.sync.dma_start(x_list[:], offs)
         nc.sync.dma_start(out=x_planes[0][:], in_=xT_planes[0])
+        load_head_rows(z_rows, wgt2)
+        nc.sync.dma_start(out=z_rows[64 : 64 + TILES, :], in_=b.rearrange("(c p) -> c p", p=P))
         nc.sync.dma_start(out=x_planes[1][:], in_=xT_planes[1])
         nc.sync.dma_start(z_list[:], offs2)
         nc.sync.dma_start(out=x_planes[2][:], in_=xT_planes[2])
         nc.sync.dma_start(out=x_planes[3][:], in_=xT_planes[3])
-        for t in range(PACK):
-            if t == 2:
-                nc.sync.dma_start(out=wb_raw[:], in_=wb.rearrange("(p t) n -> p t n", t=PACK))
+        nc.sync.dma_start(out=z_planes[0][:], in_=zT_planes[0])
+        nc.sync.dma_start(out=wb_raw[:], in_=wb.rearrange("(p t) n -> p t n", t=PACK))
+        for t in range(1, PACK):
+            if t == PACK - 1:
+                nc.sync.dma_start(out=wa_codes[:].bitcast(I32), in_=wa_words[0].bitcast(I32))
             nc.sync.dma_start(out=z_planes[t][:], in_=zT_planes[t])
-        nc.sync.dma_start(out=wa_codes[:].bitcast(I32), in_=wa_words[0].bitcast(I32))
-        nc.sync.dma_start(out=bias_rows[: N // P, :], in_=b.rearrange("(c p) -> c p", p=P))
         for q in range(4):
             nc.gpsimd.dma_start(
                 out=wa_plane[32 * q : 32 * q + 4, :].bitcast(I32),
                 in_=wa_scales[0, 4 * q : 4 * q + 4, :].bitcast(I32),
             )
 
-        turned = bank(0, [P, P], "turned")
-        nc.tensor.transpose(turned[:], head_rows[:], ident[:])
         x_weights = keep.tile([P, J], F32, name="x_weights")
-        zg_early = keep.tile([P, PACK, HALF], F32, name="zg_early")
-        pitch = 640
-        late2 = keep.tile([P, PACK * pitch], F32, name="late2", align_bytes=64)
-        late3 = keep.tile([P, PACK * CHUNK], F32, name="late3", align_bytes=64)
-        zg = [
-            zg_early[:, :, :CHUNK],
-            zg_early[:, :, CHUNK:],
-            late2[:].rearrange("p (t w) -> p t w", t=PACK)[:, :, :CHUNK],
-            late3[:].rearrange("p (t w) -> p t w", t=PACK),
-        ]
-        z_weights_late = keep.tile([P, HALF], F32, name="z_weights_late")
-        lap = 128
-        z_weights = [late2[:, CHUNK : CHUNK + HALF], z_weights_late[:]]
-        z_grouped = [
-            late2[:, 3 * pitch + 64 - HALF : 3 * pitch + 64],
-            late3[:, CHUNK + lap : CHUNK + lap + HALF],
-            keep.tile([P, HALF], F32, name="z_grouped2", align_bytes=64)[:],
-            keep.tile([P, HALF], F32, name="z_grouped3", align_bytes=64)[:],
-        ]
-        z_grouped = [g.bitcast(BF16).rearrange("p (c t) -> p c t", t=PACK) for g in z_grouped]
-        by_head = turned[:].rearrange("j (s h c) -> j s c h", s=2, h=HEADS)
-        pieces = [
-            (0, 0, 2, x_weights[:, :CHUNK]),
-            (0, 2, 4, x_weights[:, CHUNK:HALF]),
-            (0, 4, 6, x_weights[:, HALF : HALF + CHUNK]),
-            (0, 6, 8, x_weights[:, HALF + CHUNK :]),
-            (1, 0, 4, z_weights[0]),
-            (1, 4, 8, z_weights[1]),
-        ]
-        for i, (s, c0, c1, dst) in enumerate(pieces):
-            copy = nc.vector.tensor_copy if s == 0 else nc.scalar.copy
-            count = c1 - c0
-            spread = keep.tile([P, count, HEADS, GROUP], F32, name="spread%d" % i, tag="spread%d" % min(i, 3))
-            copy(out=spread[:], in_=by_head[:, s, c0:c1, :].unsqueeze(3).to_broadcast([P, count, HEADS, GROUP]))
-            back = bank(1 + i, [P, count, P], "back%d" % i)
-            for c in range(count):
-                nc.tensor.transpose(back[:, c, :], spread[:, c].rearrange("j h r -> j (h r)"), ident[:])
-            nc.scalar.copy(out=dst, in_=back[:].rearrange("p c j -> p (c j)"))
+        z_weights = keep.tile([P, J], F32, name="z_weights")
 
-        def gather_x(t, lo, hi):
-            nc.vector.tensor_tensor(
-                xg[:, t, lo:hi], x_planes[t][:].indirect(x_list[:, lo // 16 : hi // 16]), x_weights[:, lo:hi], ALU.mult
-            )
+        def spread_weights(name, turned, first_bank, count, copy, weights, tags):
+            by_head = turned[:, :64].rearrange("j (h c) -> j c h", h=HEADS)
+            for i in range(HEADS // count):
+                spread = keep.tile([P, count, HEADS, GROUP], F32, name="%s_spread%d" % (name, i), tag=tags[i], align_bytes=64)
+                copy(
+                    out=spread[:],
+                    in_=by_head[:, count * i : count * (i + 1), :].unsqueeze(3).to_broadcast([P, count, HEADS, GROUP]),
+                )
+                back = bank(first_bank + i, [P, count, P], "%s_back%d" % (name, i))
+                for c in range(count):
+                    nc.tensor.transpose(back[:, c, :], spread[:, c].rearrange("j h r -> j (h r)"), ident[:])
+                nc.scalar.copy(
+                    out=weights[:, count * P * i : count * P * (i + 1)], in_=back[:].rearrange("p c j -> p (c j)")
+                )
 
-        def gather_z(t, lo, hi):
-            u = lo // HALF
-            cols = slice(lo - u * HALF, hi - u * HALF)
-            nc.vector.tensor_tensor(
-                zg_early[:, t, cols] if u == 0 else zg[lo // CHUNK][:, t, lo % CHUNK : lo % CHUNK + hi - lo],
-                z_planes[t][:].indirect(z_list[:, lo // 16 : hi // 16]),
-                z_weights[u][:, cols],
-                ALU.mult,
-            )
+        x_turned = bank(0, [P, P], "x_turned")
+        nc.tensor.transpose(x_turned[:], x_rows[:], ident[:])
+        spread_weights("x", x_turned, 1, 2, nc.vector.tensor_copy, x_weights, ["s0", "s1", "s2", "s3"])
+        z_turned = bank(4, [P, P], "z_turned")
+        nc.tensor.transpose(z_turned[:], z_rows[:], ident[:])
+        spread_weights("z", z_turned, 6, 4, nc.scalar.copy, z_weights, ["s2", "s3"])
+        nc.scalar.copy(out=bias[:], in_=z_turned[:, 64 : 64 + TILES])
 
-        def quantize(name, grouped, width):
-            codes = keep.tile([P, width], U32, name=name + "_codes", align_bytes=64)
+        def gather(dst, plane, places, weights, lo, hi):
+            nc.vector.tensor_tensor(dst, plane[:].indirect(places[:, lo // 16 : hi // 16]), weights[:, lo:hi], ALU.mult)
+
+        def quantize(name, grouped, width, pool=keep, **place):
+            codes = pool.tile([P, width], U32, name=name + "_codes", align_bytes=64, **place)
             plane = keep.tile([P, width], U8, name=name + "_plane", align_bytes=64)
             nc.vector.quantize_mx(
                 out=codes[:].bitcast(FP8X4), scales=plane[:], in_=grouped.rearrange("p c t -> p (c t)")
@@ -158,133 +141,120 @@ def tile_list_absd_gelu_kernel(
             return codes, plane
 
         xg = keep.tile([P, PACK, J], F32, name="xg")
+        x_grouped = keep.tile([P, J, PACK], BF16, name="x_grouped", tag="s3", align_bytes=64)
         for t in range(PACK):
-            cuts = ((0, CHUNK, HALF, HALF + CHUNK, J), (0, J), (0, J), (0, HALF, J))[t]
-            for lo, hi in zip(cuts, cuts[1:]):
-                gather_x(t, lo, hi)
-        x_grouped = []
-        for u in range(2):
-            grouped = keep.tile([P, HALF, PACK], BF16, name="x_grouped%d" % u, align_bytes=64)
-            nc.scalar.copy(out=woven_out(grouped[:]), in_=woven(xg[:, :, HALF * u : HALF * (u + 1)]))
-            x_grouped.append(grouped)
-
-        gather_z(0, 0, HALF)
-        gather_z(0, HALF, HALF + CHUNK)
-        gather_z(0, HALF + CHUNK, J)
+            step = PIECE if t in (0, PACK - 1) else J
+            for lo in range(0, J, step):
+                gather(xg[:, t, lo : lo + step], x_planes[t], x_list, x_weights, lo, lo + step)
+            if t % 2:
+                for c in range(CHUNKS):
+                    nc.scalar.copy(
+                        out=x_grouped[:, c * PIECE : (c + 1) * PIECE, t - 1 : t + 1],
+                        in_=by_column(xg[:, t - 1 : t + 1, c * PIECE : (c + 1) * PIECE]),
+                    )
 
         wb_grouped = keep.tile([P, N, PACK], BF16, name="wb_grouped", align_bytes=64)
         nc.scalar.activation(woven_out(wb_grouped[:]), woven(wb_raw[:]), ACT.Copy, scale=-1.0)
 
-        x_q = [quantize("x%d" % u, x_grouped[u][:], HALF) for u in range(2)]
-        sums = {}
+        z_grouped = [
+            keep.tile([P, PIECE, PACK], BF16, name="z_grouped%d" % c, align_bytes=64)[:] for c in range(CHUNKS)
+        ]
+        late_at = (0, 4096, 0, 5632)
+        x_codes_at = {2: 3584, 3: 4608}
+        z_late = []
+        z_early = keep.tile([P, 2, J], F32, name="z_early")
+        gather(z_early[:, 0, :], z_planes[0], z_list, z_weights, 0, J)
+        early = EARLY_CHUNKS * PIECE
+        x_q = [quantize("x0", x_grouped[:, :early, :], early, tag="z_plane0")]
+        for c in range(CHUNKS):
+            lo = c * PIECE
+            gather(z_early[:, 1, lo : lo + PIECE], z_planes[1], z_list, z_weights, lo, lo + PIECE)
+            nc.scalar.copy(out=z_grouped[c][:, :, :2], in_=by_column(z_early[:, :, lo : lo + PIECE]))
 
-        def open_sums(c):
-            codes, plane = x_q[c * CHUNK // HALF]
-            for pair in range(2):
-                acc = bank(2 * (c % 2) + pair, [P, 2, CHUNK], "sum%d%d" % (c, pair))
-                sums[c, pair] = acc
-                for m in range(2):
-                    nt = 2 * pair + m
-                    for v in range(CHUNK // P):
-                        col = c * CHUNK % HALF + v * P
-                        nc.tensor.matmul_mx(
-                            out=acc[:, m, v * P : (v + 1) * P],
-                            lhsT=wa_codes[:, 2 * P * nt : 2 * P * (nt + 1)].bitcast(FP4X4),
-                            lhsT_scale=wa_plane[:, P * nt : P * (nt + 1)],
-                            rhs=codes[:, col : col + P].bitcast(FP8X4),
-                            rhs_scale=plane[:, col : col + P],
-                            start=(m == 0 and v == 0),
-                            stop=False,
-                        )
+        wb_codes, wb_plane = quantize("wb", wb_grouped[:], N, tag="z_plane1")
 
-        open_sums(0)
-        gather_z(1, 0, HALF)
-        gather_z(2, 0, HALF)
-        wb_codes, wb_plane = quantize("wb", wb_grouped[:], N)
+        sums = [bank(s, [P, TILES, P] if s < 2 else [P, 2, PIECE], "sum%d" % s) for s in range(2 * CHUNKS)]
+
+        def passes(c, at, width, weights, moving, opening):
+            codes, plane = moving
+            for nt in range(TILES):
+                acc = sums[at // P][:, nt, :] if c == 0 else sums[2 * c + nt // 2][:, nt % 2, :]
+                per_bank = TILES if c == 0 else 2
+                nc.tensor.matmul_mx(
+                    out=acc,
+                    lhsT=weights(nt)[0],
+                    lhsT_scale=weights(nt)[1],
+                    rhs=codes.bitcast(FP8X4),
+                    rhs_scale=plane,
+                    start=(opening and nt % per_bank == 0),
+                    stop=(not opening and nt % per_bank == per_bank - 1),
+                )
+
+        def wa_tile(nt):
+            return wa_codes[:, 2 * P * nt : 2 * P * (nt + 1)].bitcast(FP4X4), wa_plane[:, P * nt : P * (nt + 1)]
+
+        def wb_tile(nt):
+            return wb_codes[:, P * nt : P * (nt + 1)].bitcast(FP8X4), wb_plane[:, P * nt : P * (nt + 1)]
+
+        def gather_late(t, c, at, width):
+            if len(z_late) == c:
+                z_late.append(over.tile([P, 2, PIECE], F32, name="z_late%d" % c, align_bytes=64, offset=late_at[c])[:])
+            lo = c * PIECE + at
+            gather(z_late[c][:, t - 2, at : at + width], z_planes[t], z_list, z_weights, lo, lo + width)
+
+        z_q = []
+        for c in range(EARLY_CHUNKS):
+            gather_late(2, c, 0, PIECE)
+        for c in range(CHUNKS):
+            width = P if c == 0 else PIECE
+            for at in range(0, PIECE, width):
+                if c >= EARLY_CHUNKS:
+                    gather_late(2, c, at, width)
+                gather_late(3, c, at, width)
+                if c >= EARLY_CHUNKS:
+                    x_now = quantize("x%d" % c, x_grouped[:, c * PIECE : (c + 1) * PIECE, :], PIECE, over, offset=x_codes_at[c])
+                    places = slice(0, PIECE)
+                else:
+                    x_now = x_q[0]
+                    places = slice(c * PIECE + at, c * PIECE + at + width)
+                passes(c, at, width, wa_tile, (x_now[0][:, places], x_now[1][:, places]), True)
+                copy = nc.scalar.copy if c < EARLY_CHUNKS else nc.vector.tensor_copy
+                copy(out=z_grouped[c][:, at : at + width, 2:], in_=by_column(z_late[c][:, :, at : at + width]))
+                codes, plane = quantize("z%d_%d" % (c, at), z_grouped[c][:, at : at + width, :], width)
+                z_q.append(codes)
+                passes(c, at, width, wb_tile, (codes[:], plane[:]), False)
 
         out_tiles = out.rearrange("(nt p) j -> p nt j", p=P)
+        first_mags = keep.tile([P, TILES, PIECE], F32, name="first_mags")
+        mags = [first_mags[:, :2, :], first_mags[:, 2:, :]]
+        mags.extend(keep.tile([P, 2, PIECE], F32, name="mag%d" % s)[:] for s in range(2, len(sums)))
 
-        def gather_chunk(t, c):
-            gather_z(t, c * CHUNK, (c + 1) * CHUNK)
-
-        def parts(c):
-            width = P if c == CHUNKS - 1 else CHUNK
-            return [slice(lo, lo + width) for lo in range(0, CHUNK, width)]
-
-        def weave(c):
-            copy = nc.scalar.copy if c < 2 else nc.vector.tensor_copy
-            for cols in parts(c):
-                copy(out=woven_out(z_grouped[c][:, cols, :]), in_=woven(zg[c][:, :, cols]))
-
-        def finish(c):
-            operands = [
-                (cols, quantize("z%d_%d" % (c, cols.start), z_grouped[c][:, cols, :], cols.stop - cols.start))
-                for cols in parts(c)
-            ]
-            mags = []
-            for pair in range(2):
-                acc = sums[c, pair]
-                for cols, (codes, plane) in operands:
-                    for m in range(2):
-                        nt = 2 * pair + m
-                        nc.tensor.matmul_mx(
-                            out=acc[:, m, cols],
-                            lhsT=wb_codes[:, P * nt : P * (nt + 1)].bitcast(FP8X4),
-                            lhsT_scale=wb_plane[:, P * nt : P * (nt + 1)],
-                            rhs=codes[:].bitcast(FP8X4),
-                            rhs_scale=plane[:],
-                            start=False,
-                            stop=(m == 1 and cols.stop == CHUNK),
-                        )
-                mag = keep.tile([P, 2 * CHUNK], F32, name="mag%d%d" % (c, pair))
-                flat = acc[:].rearrange("p m j -> p (m j)")
-                if c == CHUNKS - 1:
-                    neg = keep.tile([P, 2 * CHUNK], F32, name="neg%d" % pair)
-                    tiles = (slice(0, CHUNK), slice(CHUNK, 2 * CHUNK))
-                    for cols in tiles:
-                        nc.vector.tensor_scalar(neg[:, cols], flat[:, cols], -1.0, None, ALU.mult)
-                    for cols in tiles:
-                        nc.vector.tensor_tensor(mag[:, cols], neg[:, cols], flat[:, cols], ALU.max)
-                else:
-                    nc.scalar.activation(mag[:], flat, ACT.Abs)
-                mags.append(mag)
-            for pair in range(2):
-                res = keep.tile([P, 2, CHUNK], F32, name="res%d%d" % (c, pair))
+        def magnitude(s):
+            if s < 2:
+                nc.scalar.activation(first_mags[:, :, s * P : (s + 1) * P], sums[s][:], ACT.Abs)
+            elif s < len(sums) - VECTOR_ABS:
+                nc.scalar.activation(mags[s], sums[s][:], ACT.Abs)
+            else:
+                neg = keep.tile([P, 2, PIECE], F32, name="neg%d" % s)
                 for m in range(2):
-                    nt = 2 * pair + m
-                    nc.scalar.activation(
-                        res[:, m, :],
-                        mags[pair][:, m * CHUNK : (m + 1) * CHUNK],
-                        ACT.Gelu_apprx_tanh,
-                        bias=bias[:, nt : nt + 1],
-                    )
-                    if (c, pair) == (CHUNKS - 1, 1):
-                        nc.sync.dma_start(out=out_tiles[:, nt, c * CHUNK : (c + 1) * CHUNK], in_=res[:, m, :])
-                if (c, pair) != (CHUNKS - 1, 1):
-                    nc.sync.dma_start(
-                        out=out_tiles[:, 2 * pair : 2 * pair + 2, c * CHUNK : (c + 1) * CHUNK], in_=res[:]
-                    )
+                    nc.vector.tensor_scalar(neg[:, m, :], sums[s][:, m, :], -1.0, None, ALU.mult)
+                for m in range(2):
+                    nc.vector.tensor_tensor(mags[s][:, m, :], neg[:, m, :], sums[s][:, m, :], ALU.max)
 
-        gather_chunk(3, 0)
-        weave(0)
-        gather_chunk(3, 1)
-        weave(1)
-        gather_chunk(1, 2)
-        bias_turned = bank(7, [P, P], "bias_turned")
-        nc.tensor.transpose(bias_turned[:], bias_rows[:], ident[:])
-        nc.scalar.copy(out=bias[:], in_=bias_turned[:, : N // P])
-        finish(0)
-        open_sums(1)
-        open_sums(2)
-        gather_chunk(2, 2)
-        gather_chunk(3, 2)
-        finish(1)
-        open_sums(3)
-        weave(2)
-        gather_chunk(1, 3)
-        finish(2)
-        gather_chunk(2, 3)
-        gather_z(3, J - CHUNK, J - P)
-        gather_z(3, J - P, J)
-        weave(3)
-        finish(3)
+        def finish(s):
+            places = slice(s // 2 * PIECE, (s // 2 + 1) * PIECE)
+            first = 2 * (s % 2)
+            res = keep.tile([P, 2, PIECE], F32, name="res%d" % s)
+            for m in range(2):
+                nt = first + m
+                nc.scalar.activation(res[:, m, :], mags[s][:, m, :], ACT.Gelu_apprx_tanh, bias=bias[:, nt : nt + 1])
+                if s == len(sums) - 1:
+                    nc.sync.dma_start(out=out_tiles[:, nt, places], in_=res[:, m, :])
+            if s < len(sums) - 1:
+                nc.sync.dma_start(out=out_tiles[:, first : first + 2, places], in_=res[:])
+
+        magnitude(0)
+        for s in range(len(sums)):
+            if s + 1 < len(sums):
+                magnitude(s + 1)
+            finish(s)

@@ -26,7 +26,7 @@ TILES = N // P
 PIECE = 256
 CHUNKS = J // PIECE
 EARLY_CHUNKS = 2
-VECTOR_ABS = 3
+VECTOR_ABS = 2
 
 
 def woven(src):

@@ -26,7 +26,7 @@ TILES = N // P
 PIECE = 256
 CHUNKS = J // PIECE
 EARLY_CHUNKS = 2
-VECTOR_ABS = 2
+VECTOR_ABS = (5, 7)
 
 
 def woven(src):
@@ -232,7 +232,7 @@ def tile_list_absd_gelu_kernel(
         def magnitude(s):
             if s < 2:
                 nc.scalar.activation(first_mags[:, :, s * P : (s + 1) * P], sums[s][:], ACT.Abs)
-            elif s < len(sums) - VECTOR_ABS:
+            elif s not in VECTOR_ABS:
                 nc.scalar.activation(mags[s], sums[s][:], ACT.Abs)
             else:
                 neg = keep.tile([P, 2, PIECE], F32, name="neg%d" % s)

@@ -26,7 +26,6 @@ TILES = N // P
 PIECE = 256
 CHUNKS = J // PIECE
 EARLY_CHUNKS = 2
-VECTOR_ABS = (5, 7)
 
 
 def woven(src):
@@ -58,7 +57,8 @@ def tile_list_absd_gelu_kernel(
         x_rows = keep.tile([P, P], F32, name="x_rows")
         z_rows = keep.tile([P, P], F32, name="z_rows")
         x_planes = [keep.tile([P, T], F32, name="x_plane%d" % t) for t in range(PACK)]
-        z_planes = [keep.tile([P, T], F32, name="z_plane%d" % t, align_bytes=64) for t in range(PACK)]
+        z_planes = [over.tile([P, T], F32, name="z_plane0", align_bytes=64, offset=8192)]
+        z_planes.extend(keep.tile([P, T], F32, name="z_plane%d" % t, align_bytes=64) for t in range(1, PACK))
         wa_codes = keep.tile([P, 2 * N], U8, name="wa_codes", align_bytes=64)
         wa_plane = keep.tile([P, N], U8, name="wa_plane", align_bytes=64)
         wb_raw = keep.tile([P, PACK, N], F32, name="wb_raw")
@@ -94,9 +94,8 @@ def tile_list_absd_gelu_kernel(
         nc.sync.dma_start(out=z_planes[0][:], in_=zT_planes[0])
         nc.sync.dma_start(out=wb_raw[:], in_=wb.rearrange("(p t) n -> p t n", t=PACK))
         for t in range(1, PACK):
-            if t == PACK - 1:
-                nc.sync.dma_start(out=wa_codes[:].bitcast(I32), in_=wa_words[0].bitcast(I32))
             nc.sync.dma_start(out=z_planes[t][:], in_=zT_planes[t])
+        nc.sync.dma_start(out=wa_codes[:].bitcast(I32), in_=wa_words[0].bitcast(I32))
         for q in range(4):
             nc.gpsimd.dma_start(
                 out=wa_plane[32 * q : 32 * q + 4, :].bitcast(I32),
@@ -143,14 +142,14 @@ def tile_list_absd_gelu_kernel(
         xg = keep.tile([P, PACK, J], F32, name="xg")
         x_grouped = keep.tile([P, J, PACK], BF16, name="x_grouped", tag="s3", align_bytes=64)
         for t in range(PACK):
-            step = PIECE if t in (0, PACK - 1) else J
+            step = (PIECE, J, J, J // 2)[t]
             for lo in range(0, J, step):
                 gather(xg[:, t, lo : lo + step], x_planes[t], x_list, x_weights, lo, lo + step)
             if t % 2:
-                for c in range(CHUNKS):
+                for lo in range(0, J, J // 2):
                     nc.scalar.copy(
-                        out=x_grouped[:, c * PIECE : (c + 1) * PIECE, t - 1 : t + 1],
-                        in_=by_column(xg[:, t - 1 : t + 1, c * PIECE : (c + 1) * PIECE]),
+                        out=x_grouped[:, lo : lo + J // 2, t - 1 : t + 1],
+                        in_=by_column(xg[:, t - 1 : t + 1, lo : lo + J // 2]),
                     )
 
         wb_grouped = keep.tile([P, N, PACK], BF16, name="wb_grouped", align_bytes=64)
@@ -159,27 +158,46 @@ def tile_list_absd_gelu_kernel(
         z_grouped = [
             keep.tile([P, PIECE, PACK], BF16, name="z_grouped%d" % c, align_bytes=64)[:] for c in range(CHUNKS)
         ]
-        late_at = (0, 4096, 0, 5632)
-        x_codes_at = {2: 3584, 3: 4608}
-        z_late = []
-        z_early = keep.tile([P, 2, J], F32, name="z_early")
-        gather(z_early[:, 0, :], z_planes[0], z_list, z_weights, 0, J)
+        z_last = keep.tile([P, PACK, PIECE], F32, name="z_last")
+        under_last = z_last[:].rearrange("p t c -> p (t c)")[:, 3 * P : 7 * P]
+        z_late = {1: under_last.rearrange("p (t c) -> p t c", t=2), 3: z_last[:, 2:, :]}
+        paired = J - PIECE
+        z_first = keep.tile([P, 2, PIECE], F32, name="z_first", align_bytes=64)
+        z_next = keep.tile([P, 2, 2 * PIECE], F32, name="z_next")
+        z_early = [z_first[:], z_next[:, :, :PIECE], z_next[:, :, PIECE:]]
+        gather(z_first[:, 0, :], z_planes[0], z_list, z_weights, 0, PIECE)
+        gather(z_next[:, 0, :], z_planes[0], z_list, z_weights, PIECE, paired)
+        gather(z_last[:, 0, :], z_planes[0], z_list, z_weights, paired, J)
         early = EARLY_CHUNKS * PIECE
-        x_q = [quantize("x0", x_grouped[:, :early, :], early, tag="z_plane0")]
-        for c in range(CHUNKS):
-            lo = c * PIECE
-            gather(z_early[:, 1, lo : lo + PIECE], z_planes[1], z_list, z_weights, lo, lo + PIECE)
-            nc.scalar.copy(out=z_grouped[c][:, :, :2], in_=by_column(z_early[:, :, lo : lo + PIECE]))
+        x_q = [quantize("x0", x_grouped[:, :early, :], early, over, offset=8192)]
+        x_q.append(quantize("x2", x_grouped[:, early : early + PIECE, :], PIECE, over, offset=8192 + 4 * early))
+        for c in range(CHUNKS - 1):
+            if c == 0:
+                gather(z_first[:, 1, :], z_planes[1], z_list, z_weights, 0, PIECE)
+            elif c == 1:
+                gather(z_next[:, 1, :], z_planes[1], z_list, z_weights, PIECE, paired)
+            nc.scalar.copy(out=z_grouped[c][:, :, :2], in_=by_column(z_early[c]))
 
-        wb_codes, wb_plane = quantize("wb", wb_grouped[:], N, tag="z_plane1")
+        wb_codes, wb_plane = quantize("wb", wb_grouped[:], N, tag="z_first")
 
-        sums = [bank(s, [P, TILES, P] if s < 2 else [P, 2, PIECE], "sum%d" % s) for s in range(2 * CHUNKS)]
+        sums = {}
+
+        def sum_of(c, at, nt):
+            if c == 0:
+                key, per_bank, number = (c, at), TILES, at // P
+            elif c < CHUNKS - 1:
+                key, per_bank, number = (c, nt // 2), 2, 2 * c + nt // 2
+            else:
+                key, per_bank, number = (c, nt), 1, (6, 7, 0, 1)[nt]
+            if key not in sums:
+                sums[key] = bank(number, [P, per_bank, P if c == 0 else PIECE], "sum%d_%d" % key)
+            return sums[key], per_bank
 
         def passes(c, at, width, weights, moving, opening):
             codes, plane = moving
             for nt in range(TILES):
-                acc = sums[at // P][:, nt, :] if c == 0 else sums[2 * c + nt // 2][:, nt % 2, :]
-                per_bank = TILES if c == 0 else 2
+                held, per_bank = sum_of(c, at, nt)
+                acc = held[:, nt % per_bank, :]
                 nc.tensor.matmul_mx(
                     out=acc,
                     lhsT=weights(nt)[0],
@@ -197,8 +215,8 @@ def tile_list_absd_gelu_kernel(
             return wb_codes[:, P * nt : P * (nt + 1)].bitcast(FP8X4), wb_plane[:, P * nt : P * (nt + 1)]
 
         def gather_late(t, c, at, width):
-            if len(z_late) == c:
-                z_late.append(over.tile([P, 2, PIECE], F32, name="z_late%d" % c, align_bytes=64, offset=late_at[c])[:])
+            if c not in z_late:
+                z_late[c] = keep.tile([P, 2, PIECE], F32, name="z_late%d" % c, tag="z_late")[:]
             lo = c * PIECE + at
             gather(z_late[c][:, t - 2, at : at + width], z_planes[t], z_list, z_weights, lo, lo + width)
 
@@ -208,18 +226,26 @@ def tile_list_absd_gelu_kernel(
         for c in range(CHUNKS):
             width = P if c == 0 else PIECE
             for at in range(0, PIECE, width):
+                if c == CHUNKS - 1:
+                    gather(z_last[:, 1, :], z_planes[1], z_list, z_weights, paired, J)
                 if c >= EARLY_CHUNKS:
                     gather_late(2, c, at, width)
                 gather_late(3, c, at, width)
-                if c >= EARLY_CHUNKS:
-                    x_now = quantize("x%d" % c, x_grouped[:, c * PIECE : (c + 1) * PIECE, :], PIECE, over, offset=x_codes_at[c])
+                if c == EARLY_CHUNKS:
+                    x_now = x_q[1]
+                    places = slice(0, PIECE)
+                elif c > EARLY_CHUNKS:
+                    x_now = quantize("x%d" % c, x_grouped[:, c * PIECE : (c + 1) * PIECE, :], PIECE, tag="z_grouped1")
                     places = slice(0, PIECE)
                 else:
                     x_now = x_q[0]
                     places = slice(c * PIECE + at, c * PIECE + at + width)
                 passes(c, at, width, wa_tile, (x_now[0][:, places], x_now[1][:, places]), True)
                 copy = nc.scalar.copy if c < EARLY_CHUNKS else nc.vector.tensor_copy
-                copy(out=z_grouped[c][:, at : at + width, 2:], in_=by_column(z_late[c][:, :, at : at + width]))
+                if c == CHUNKS - 1:
+                    copy(out=woven_out(z_grouped[c]), in_=woven(z_last[:]))
+                else:
+                    copy(out=z_grouped[c][:, at : at + width, 2:], in_=by_column(z_late[c][:, :, at : at + width]))
                 codes, plane = quantize("z%d_%d" % (c, at), z_grouped[c][:, at : at + width, :], width)
                 z_q.append(codes)
                 passes(c, at, width, wb_tile, (codes[:], plane[:]), False)
@@ -227,19 +253,31 @@ def tile_list_absd_gelu_kernel(
         out_tiles = out.rearrange("(nt p) j -> p nt j", p=P)
         first_mags = keep.tile([P, TILES, PIECE], F32, name="first_mags")
         mags = [first_mags[:, :2, :], first_mags[:, 2:, :]]
-        mags.extend(keep.tile([P, 2, PIECE], F32, name="mag%d" % s)[:] for s in range(2, len(sums)))
+        mags.extend(keep.tile([P, 2, PIECE], F32, name="mag%d" % s)[:] for s in range(2, 2 * CHUNKS))
+
+        def on_vector(mag, parts, name):
+            neg = keep.tile([P, len(parts), PIECE], F32, name=name)
+            for m, part in enumerate(parts):
+                nc.vector.tensor_scalar(neg[:, m, :], part, -1.0, None, ALU.mult)
+            for m, part in enumerate(parts):
+                nc.vector.tensor_tensor(mag[m], neg[:, m, :], part, ALU.max)
 
         def magnitude(s):
-            if s < 2:
-                nc.scalar.activation(first_mags[:, :, s * P : (s + 1) * P], sums[s][:], ACT.Abs)
-            elif s not in VECTOR_ABS:
-                nc.scalar.activation(mags[s], sums[s][:], ACT.Abs)
+            c, pair = divmod(s, 2)
+            if c == 0:
+                nc.scalar.activation(first_mags[:, :, s * P : (s + 1) * P], sums[c, s * P][:], ACT.Abs)
+            elif c == CHUNKS - 1:
+                if pair == 0:
+                    nc.scalar.activation(mags[s][:, 0, :], sums[c, 0][:, 0, :], ACT.Abs)
+                    on_vector(
+                        [mags[s][:, 1, :], mags[s + 1][:, 0, :], mags[s + 1][:, 1, :]],
+                        [sums[c, nt][:, 0, :] for nt in range(1, TILES)],
+                        "neg_last",
+                    )
+            elif s == 2 * CHUNKS - 3:
+                on_vector([mags[s][:, m, :] for m in range(2)], [sums[c, pair][:, m, :] for m in range(2)], "neg")
             else:
-                neg = keep.tile([P, 2, PIECE], F32, name="neg%d" % s)
-                for m in range(2):
-                    nc.vector.tensor_scalar(neg[:, m, :], sums[s][:, m, :], -1.0, None, ALU.mult)
-                for m in range(2):
-                    nc.vector.tensor_tensor(mags[s][:, m, :], neg[:, m, :], sums[s][:, m, :], ALU.max)
+                nc.scalar.activation(mags[s], sums[c, pair][:], ACT.Abs)
 
         def finish(s):
             places = slice(s // 2 * PIECE, (s // 2 + 1) * PIECE)
@@ -248,13 +286,13 @@ def tile_list_absd_gelu_kernel(
             for m in range(2):
                 nt = first + m
                 nc.scalar.activation(res[:, m, :], mags[s][:, m, :], ACT.Gelu_apprx_tanh, bias=bias[:, nt : nt + 1])
-                if s == len(sums) - 1:
+                if s == 2 * CHUNKS - 1:
                     nc.sync.dma_start(out=out_tiles[:, nt, places], in_=res[:, m, :])
-            if s < len(sums) - 1:
+            if s < 2 * CHUNKS - 1:
                 nc.sync.dma_start(out=out_tiles[:, first : first + 2, places], in_=res[:])
 
         magnitude(0)
-        for s in range(len(sums)):
-            if s + 1 < len(sums):
+        for s in range(2 * CHUNKS):
+            if s + 1 < 2 * CHUNKS:
                 magnitude(s + 1)
             finish(s)

@@ -25,7 +25,6 @@ GROUP = 16
 TILES = N // P
 PIECE = 256
 CHUNKS = J // PIECE
-EARLY_CHUNKS = 2
 
 
 def woven(src):
@@ -57,8 +56,7 @@ def tile_list_absd_gelu_kernel(
         x_rows = keep.tile([P, P], F32, name="x_rows")
         z_rows = keep.tile([P, P], F32, name="z_rows")
         x_planes = [keep.tile([P, T], F32, name="x_plane%d" % t) for t in range(PACK)]
-        z_planes = [over.tile([P, T], F32, name="z_plane0", align_bytes=64, offset=8192)]
-        z_planes.extend(keep.tile([P, T], F32, name="z_plane%d" % t, align_bytes=64) for t in range(1, PACK))
+        z_planes = [keep.tile([P, T], F32, name="z_plane%d" % t) for t in range(PACK)]
         wa_codes = keep.tile([P, 2 * N], U8, name="wa_codes", align_bytes=64)
         wa_plane = keep.tile([P, N], U8, name="wa_plane", align_bytes=64)
         wb_raw = keep.tile([P, PACK, N], F32, name="wb_raw")
@@ -76,6 +74,7 @@ def tile_list_absd_gelu_kernel(
 
         xT_planes = xT.rearrange("(p t) n -> t p n", t=PACK)
         zT_planes = zT.rearrange("(p t) n -> t p n", t=PACK)
+        wb_rows = wb.rearrange("(p t) n -> p t n", t=PACK)
 
         def load_head_rows(rows, w):
             nc.sync.dma_start(
@@ -92,10 +91,11 @@ def tile_list_absd_gelu_kernel(
         nc.sync.dma_start(out=x_planes[2][:], in_=xT_planes[2])
         nc.sync.dma_start(out=x_planes[3][:], in_=xT_planes[3])
         nc.sync.dma_start(out=z_planes[0][:], in_=zT_planes[0])
-        nc.sync.dma_start(out=wb_raw[:], in_=wb.rearrange("(p t) n -> p t n", t=PACK))
-        for t in range(1, PACK):
+        nc.sync.dma_start(out=wb_raw[:], in_=wb_rows)
+        for t in range(1, PACK - 1):
             nc.sync.dma_start(out=z_planes[t][:], in_=zT_planes[t])
         nc.sync.dma_start(out=wa_codes[:].bitcast(I32), in_=wa_words[0].bitcast(I32))
+        nc.sync.dma_start(out=z_planes[PACK - 1][:], in_=zT_planes[PACK - 1])
         for q in range(4):
             nc.gpsimd.dma_start(
                 out=wa_plane[32 * q : 32 * q + 4, :].bitcast(I32),
@@ -131,6 +131,9 @@ def tile_list_absd_gelu_kernel(
         def gather(dst, plane, places, weights, lo, hi):
             nc.vector.tensor_tensor(dst, plane[:].indirect(places[:, lo // 16 : hi // 16]), weights[:, lo:hi], ALU.mult)
 
+        def gather_z(dst, t, lo, hi):
+            gather(dst, z_planes[t], z_list, z_weights, lo, hi)
+
         def quantize(name, grouped, width, pool=keep, **place):
             codes = pool.tile([P, width], U32, name=name + "_codes", align_bytes=64, **place)
             plane = keep.tile([P, width], U8, name=name + "_plane", align_bytes=64)
@@ -139,7 +142,7 @@ def tile_list_absd_gelu_kernel(
             )
             return codes, plane
 
-        xg = keep.tile([P, PACK, J], F32, name="xg")
+        xg = over.tile([P, PACK, J], F32, name="xg", align_bytes=64, offset=0)
         x_grouped = keep.tile([P, J, PACK], BF16, name="x_grouped", tag="s3", align_bytes=64)
         for t in range(PACK):
             step = (PIECE, J, J, J // 2)[t]
@@ -152,147 +155,171 @@ def tile_list_absd_gelu_kernel(
                         in_=by_column(xg[:, t - 1 : t + 1, lo : lo + J // 2]),
                     )
 
+        def quantize_x(c, count, offset):
+            width = count * PIECE
+            return quantize("x%d" % c, x_grouped[:, c * PIECE : c * PIECE + width, :], width, over, offset=offset)
+
         wb_grouped = keep.tile([P, N, PACK], BF16, name="wb_grouped", align_bytes=64)
         nc.scalar.activation(woven_out(wb_grouped[:]), woven(wb_raw[:]), ACT.Copy, scale=-1.0)
 
-        z_grouped = [
-            keep.tile([P, PIECE, PACK], BF16, name="z_grouped%d" % c, align_bytes=64)[:] for c in range(CHUNKS)
-        ]
-        z_last = keep.tile([P, PACK, PIECE], F32, name="z_last")
-        under_last = z_last[:].rearrange("p t c -> p (t c)")[:, 3 * P : 7 * P]
-        z_late = {1: under_last.rearrange("p (t c) -> p t c", t=2), 3: z_last[:, 2:, :]}
-        paired = J - PIECE
+        zg0 = keep.tile([P, PIECE, PACK], BF16, name="zg0", align_bytes=64)
+        zg1 = keep.tile([P, PIECE, PACK], BF16, name="zg1", align_bytes=64)
+        zg23 = keep.tile([P, 2 * PIECE, PACK], BF16, name="zg23", align_bytes=64)
+        z_grouped = [zg0[:], zg1[:], zg23[:, :PIECE, :], zg23[:, PIECE:, :]]
         z_first = keep.tile([P, 2, PIECE], F32, name="z_first", align_bytes=64)
-        z_next = keep.tile([P, 2, 2 * PIECE], F32, name="z_next")
-        z_early = [z_first[:], z_next[:, :, :PIECE], z_next[:, :, PIECE:]]
-        gather(z_first[:, 0, :], z_planes[0], z_list, z_weights, 0, PIECE)
-        gather(z_next[:, 0, :], z_planes[0], z_list, z_weights, PIECE, paired)
-        gather(z_last[:, 0, :], z_planes[0], z_list, z_weights, paired, J)
-        early = EARLY_CHUNKS * PIECE
-        x_q = [quantize("x0", x_grouped[:, :early, :], early, over, offset=8192)]
-        x_q.append(quantize("x2", x_grouped[:, early : early + PIECE, :], PIECE, over, offset=8192 + 4 * early))
-        for c in range(CHUNKS - 1):
-            if c == 0:
-                gather(z_first[:, 1, :], z_planes[1], z_list, z_weights, 0, PIECE)
-            elif c == 1:
-                gather(z_next[:, 1, :], z_planes[1], z_list, z_weights, PIECE, paired)
-            nc.scalar.copy(out=z_grouped[c][:, :, :2], in_=by_column(z_early[c]))
-
-        wb_codes, wb_plane = quantize("wb", wb_grouped[:], N, tag="z_first")
+        z_rest = keep.tile([P, 2, J - PIECE], F32, name="z_rest")
+        gather_z(z_first[:, 0, :], 0, 0, PIECE)
+        gather_z(z_rest[:, 0, :], 0, PIECE, J)
+        x_early = quantize_x(0, 2, 0)
+        x_q = {c: tuple(a[:, c * PIECE : (c + 1) * PIECE] for a in x_early) for c in range(2)}
+        x_q[2] = quantize_x(2, 1, 8 * PIECE)
+        gather_z(z_first[:, 1, :], 1, 0, PIECE)
+        nc.scalar.copy(out=zg0[:, :, :2], in_=by_column(z_first[:]))
+        gather_z(z_rest[:, 1, :PIECE], 1, PIECE, 2 * PIECE)
+        nc.scalar.copy(out=zg1[:, :, :2], in_=by_column(z_rest[:, :, :PIECE]))
+        gather_z(z_rest[:, 1, PIECE:], 1, 2 * PIECE, J)
+        nc.scalar.copy(out=zg23[:, :, :2], in_=by_column(z_rest[:, :, PIECE:]))
+        wb_q = [quantize("wb_lo", wb_grouped[:, : N // 2, :], N // 2, tag="z_first")]
 
         sums = {}
 
-        def sum_of(c, at, nt):
-            if c == 0:
-                key, per_bank, number = (c, at), TILES, at // P
-            elif c < CHUNKS - 1:
-                key, per_bank, number = (c, nt // 2), 2, 2 * c + nt // 2
-            else:
-                key, per_bank, number = (c, nt), 1, (6, 7, 0, 1)[nt]
-            if key not in sums:
-                sums[key] = bank(number, [P, per_bank, P if c == 0 else PIECE], "sum%d_%d" % key)
-            return sums[key], per_bank
-
-        def passes(c, at, width, weights, moving, opening):
+        def passes(key, number, tiles, weights, moving, opening, at=0, closing=True):
             codes, plane = moving
-            for nt in range(TILES):
-                held, per_bank = sum_of(c, at, nt)
-                acc = held[:, nt % per_bank, :]
+            width = codes.shape[1]
+            if opening:
+                sums[key] = bank(number, [P, len(tiles), width], "sum_" + key)
+            for m, nt in enumerate(tiles):
                 nc.tensor.matmul_mx(
-                    out=acc,
+                    out=sums[key][:, m, at : at + width],
                     lhsT=weights(nt)[0],
                     lhsT_scale=weights(nt)[1],
                     rhs=codes.bitcast(FP8X4),
                     rhs_scale=plane,
-                    start=(opening and nt % per_bank == 0),
-                    stop=(not opening and nt % per_bank == per_bank - 1),
+                    start=(opening and m == 0),
+                    stop=(closing and not opening and m == len(tiles) - 1),
                 )
 
         def wa_tile(nt):
             return wa_codes[:, 2 * P * nt : 2 * P * (nt + 1)].bitcast(FP4X4), wa_plane[:, P * nt : P * (nt + 1)]
 
         def wb_tile(nt):
-            return wb_codes[:, P * nt : P * (nt + 1)].bitcast(FP8X4), wb_plane[:, P * nt : P * (nt + 1)]
+            codes, plane = wb_q[nt // 2]
+            at = P * (nt % 2)
+            return codes[:, at : at + P].bitcast(FP8X4), plane[:, at : at + P]
 
-        def gather_late(t, c, at, width):
-            if c not in z_late:
-                z_late[c] = keep.tile([P, 2, PIECE], F32, name="z_late%d" % c, tag="z_late")[:]
-            lo = c * PIECE + at
-            gather(z_late[c][:, t - 2, at : at + width], z_planes[t], z_list, z_weights, lo, lo + width)
+        def part(q, lo, hi):
+            return q[0][:, lo:hi], q[1][:, lo:hi]
 
-        z_q = []
-        for c in range(EARLY_CHUNKS):
-            gather_late(2, c, 0, PIECE)
-        for c in range(CHUNKS):
-            width = P if c == 0 else PIECE
-            for at in range(0, PIECE, width):
-                if c == CHUNKS - 1:
-                    gather(z_last[:, 1, :], z_planes[1], z_list, z_weights, paired, J)
-                if c >= EARLY_CHUNKS:
-                    gather_late(2, c, at, width)
-                gather_late(3, c, at, width)
-                if c == EARLY_CHUNKS:
-                    x_now = x_q[1]
-                    places = slice(0, PIECE)
-                elif c > EARLY_CHUNKS:
-                    x_now = quantize("x%d" % c, x_grouped[:, c * PIECE : (c + 1) * PIECE, :], PIECE, tag="z_grouped1")
-                    places = slice(0, PIECE)
-                else:
-                    x_now = x_q[0]
-                    places = slice(c * PIECE + at, c * PIECE + at + width)
-                passes(c, at, width, wa_tile, (x_now[0][:, places], x_now[1][:, places]), True)
-                copy = nc.scalar.copy if c < EARLY_CHUNKS else nc.vector.tensor_copy
-                if c == CHUNKS - 1:
-                    copy(out=woven_out(z_grouped[c]), in_=woven(z_last[:]))
-                else:
-                    copy(out=z_grouped[c][:, at : at + width, 2:], in_=by_column(z_late[c][:, :, at : at + width]))
-                codes, plane = quantize("z%d_%d" % (c, at), z_grouped[c][:, at : at + width, :], width)
-                z_q.append(codes)
-                passes(c, at, width, wb_tile, (codes[:], plane[:]), False)
+        def wa_passes(key, number, tiles, c, lo=0, hi=PIECE):
+            passes(key, number, tiles, wa_tile, part(x_q[c], lo, hi), True)
+
+        def wb_passes(key, tiles, c, lo=0, hi=PIECE):
+            passes(key, None, tiles, wb_tile, part(z_q[c], lo, hi), False)
+
+
+        late01 = keep.tile([P, 2, 2 * PIECE], F32, name="late01", align_bytes=64)
+        late = late01[:].rearrange("p t (c j) -> p (t c) j", c=2)[:, 0:4:3, :]
+        gather_z(late01[:, 0, :], 2, 0, 2 * PIECE)
+        for lo, hi in ((0, P), (P, PIECE), (PIECE, 2 * PIECE)):
+            gather_z(late01[:, 1, lo:hi], 3, lo, hi)
+        nc.scalar.copy(out=zg0[:, :P, 2:], in_=by_column(late01[:, :, :P]))
+        nc.scalar.copy(out=zg0[:, P:, 2:], in_=by_column(late01[:, :, P:PIECE]))
+        nc.scalar.copy(out=zg1[:, :, 2:], in_=by_column(late01[:, :, PIECE:]))
+
+        z0_codes = keep.tile([P, PIECE], U32, name="z0_codes", align_bytes=64)
+        z0_plane = keep.tile([P, PIECE], U8, name="z0_plane", align_bytes=64)
+        z_q = {0: (z0_codes, z0_plane)}
+        first = (("0a", 0, (0, 1), 0), ("0b", 1, (0, 1), P))
+        for key, number, tiles, lo in first:
+            wa_passes(key, number, tiles, 0, lo, lo + P)
+        wa_passes("0hi", 2, (2, 3), 0)
+        for c in (1, 2):
+            wa_passes("%dlo" % c, 1 + 2 * c, (0, 1), c)
+            wa_passes("%dhi" % c, 2 + 2 * c, (2, 3), c)
+        for lo in (0, P):
+            nc.vector.quantize_mx(
+                out=z0_codes[:, lo : lo + P].bitcast(FP8X4),
+                scales=z0_plane[:, lo : lo + P],
+                in_=zg0[:, lo : lo + P, :].rearrange("p c t -> p (c t)"),
+            )
+        for key, number, tiles, lo in first:
+            wb_passes(key, tiles, 0, lo, lo + P)
+        gather_z(late[:, 0, :], 2, 2 * PIECE, 3 * PIECE)
+        wb_q.append(quantize("wb_hi", wb_grouped[:, N // 2 :, :], N // 2, tag="zg0"))
+        wb_passes("0hi", (2, 3), 0)
+        z_q[1] = quantize("z1", z_grouped[1], PIECE)
+        wb_passes("1lo", (0, 1), 1)
+        wb_passes("1hi", (2, 3), 1)
+        gather_z(late[:, 1, :], 3, 2 * PIECE, 3 * PIECE)
+        late3 = keep.tile([P, 2, PIECE], F32, name="late3", tag="zg1", align_bytes=64)
+        gather_z(late3[:, 0, :], 2, 3 * PIECE, J)
+        nc.vector.tensor_copy(out=z_grouped[2][:, :, 2:], in_=by_column(late))
+        gather_z(late3[:, 1, :], 3, 3 * PIECE, J)
+        z_q[2] = quantize("z2", z_grouped[2], PIECE)
+        nc.vector.tensor_copy(out=z_grouped[3][:, :, 2:], in_=by_column(late3[:]))
+        x_q[3] = quantize("x3", x_grouped[:, 3 * PIECE :, :], PIECE, tag="late01")
+        z_q[3] = quantize("z3", z_grouped[3], PIECE)
 
         out_tiles = out.rearrange("(nt p) j -> p nt j", p=P)
-        first_mags = keep.tile([P, TILES, PIECE], F32, name="first_mags")
-        mags = [first_mags[:, :2, :], first_mags[:, 2:, :]]
-        mags.extend(keep.tile([P, 2, PIECE], F32, name="mag%d" % s)[:] for s in range(2, 2 * CHUNKS))
+        mags = keep.tile([P, TILES, J], F32, name="mags")
+        negs = keep.tile([P, 5, PIECE], F32, name="negs")
+        done = keep.tile([P, TILES, J], F32, name="done")
 
-        def on_vector(mag, parts, name):
-            neg = keep.tile([P, len(parts), PIECE], F32, name=name)
-            for m, part in enumerate(parts):
-                nc.vector.tensor_scalar(neg[:, m, :], part, -1.0, None, ALU.mult)
-            for m, part in enumerate(parts):
-                nc.vector.tensor_tensor(mag[m], neg[:, m, :], part, ALU.max)
+        def magnitude(key, c, first, lo=0, hi=PIECE):
+            count = sums[key].shape[1]
+            nc.scalar.activation(mags[:, first : first + count, c * PIECE + lo : c * PIECE + hi], sums[key][:], ACT.Abs)
 
-        def magnitude(s):
-            c, pair = divmod(s, 2)
-            if c == 0:
-                nc.scalar.activation(first_mags[:, :, s * P : (s + 1) * P], sums[c, s * P][:], ACT.Abs)
-            elif c == CHUNKS - 1:
-                if pair == 0:
-                    nc.scalar.activation(mags[s][:, 0, :], sums[c, 0][:, 0, :], ACT.Abs)
-                    on_vector(
-                        [mags[s][:, 1, :], mags[s + 1][:, 0, :], mags[s + 1][:, 1, :]],
-                        [sums[c, nt][:, 0, :] for nt in range(1, TILES)],
-                        "neg_last",
-                    )
-            elif s == 2 * CHUNKS - 3:
-                on_vector([mags[s][:, m, :] for m in range(2)], [sums[c, pair][:, m, :] for m in range(2)], "neg")
-            else:
-                nc.scalar.activation(mags[s], sums[c, pair][:], ACT.Abs)
+        def negate(slot, key, at):
+            nc.vector.tensor_scalar(negs[:, slot, :], sums[key][:, at, :], -1.0, None, ALU.mult)
 
-        def finish(s):
-            places = slice(s // 2 * PIECE, (s // 2 + 1) * PIECE)
-            first = 2 * (s % 2)
-            res = keep.tile([P, 2, PIECE], F32, name="res%d" % s)
-            for m in range(2):
-                nt = first + m
-                nc.scalar.activation(res[:, m, :], mags[s][:, m, :], ACT.Gelu_apprx_tanh, bias=bias[:, nt : nt + 1])
-                if s == 2 * CHUNKS - 1:
-                    nc.sync.dma_start(out=out_tiles[:, nt, places], in_=res[:, m, :])
-            if s < 2 * CHUNKS - 1:
-                nc.sync.dma_start(out=out_tiles[:, first : first + 2, places], in_=res[:])
+        def larger(slot, key, at, c, nt):
+            nc.vector.tensor_tensor(mags[:, nt, c * PIECE : (c + 1) * PIECE], negs[:, slot, :], sums[key][:, at, :], ALU.max)
 
-        magnitude(0)
-        for s in range(2 * CHUNKS):
-            if s + 1 < 2 * CHUNKS:
-                magnitude(s + 1)
-            finish(s)
+        def gelu(nt, lo, hi):
+            nc.scalar.activation(done[:, nt, lo:hi], mags[:, nt, lo:hi], ACT.Gelu_apprx_tanh, bias=bias[:, nt : nt + 1])
+
+        def store(first, count, lo, hi):
+            nc.sync.dma_start(out=out_tiles[:, first : first + count, lo:hi], in_=done[:, first : first + count, lo:hi])
+
+        def finish(c, first):
+            gelu(first, c * PIECE, (c + 1) * PIECE)
+            gelu(first + 1, c * PIECE, (c + 1) * PIECE)
+            store(first, 2, c * PIECE, (c + 1) * PIECE)
+
+        magnitude("0a", 0, 0, 0, P)
+        magnitude("0b", 0, 0, P, PIECE)
+        wb_passes("2lo", (0, 1), 2)
+        wb_passes("2hi", (2, 3), 2)
+        last = (("30", 0, (0,)), ("31", 7, (1,)), ("3hi", 1, (2, 3)))
+        for key, number, tiles in last:
+            wa_passes(key, number, tiles, 3)
+        for key, number, tiles in last:
+            wb_passes(key, tiles, 3)
+        negate(0, "2hi", 0)
+        negate(1, "2hi", 1)
+        larger(0, "2hi", 0, 2, 2)
+        larger(1, "2hi", 1, 2, 3)
+        negate(2, "31", 0)
+        negate(3, "3hi", 0)
+        larger(2, "31", 0, 3, 1)
+        negate(4, "3hi", 1)
+        larger(3, "3hi", 0, 3, 2)
+        larger(4, "3hi", 1, 3, 3)
+
+        finish(0, 0)
+        magnitude("0hi", 0, 2)
+        magnitude("1lo", 1, 0)
+        magnitude("1hi", 1, 2)
+        finish(1, 0)
+        for nt in (2, 3):
+            if nt == TILES - 1:
+                magnitude("2lo", 2, 0)
+            gelu(nt, 0, 2 * PIECE)
+            store(nt, 1, 0, 2 * PIECE)
+        finish(2, 0)
+        magnitude("30", 3, 0)
+        finish(2, 2)
+        finish(3, 0)
+        for nt in (2, 3):
+            gelu(nt, 3 * PIECE, J)
+            store(nt, 1, 3 * PIECE, J)

@@ -183,20 +183,20 @@ def tile_list_absd_gelu_kernel(
 
         sums = {}
 
-        def passes(key, number, tiles, weights, moving, opening, at=0, closing=True):
+        def passes(key, number, tiles, weights, moving, opening, lone=False):
             codes, plane = moving
             width = codes.shape[1]
             if opening:
                 sums[key] = bank(number, [P, len(tiles), width], "sum_" + key)
             for m, nt in enumerate(tiles):
                 nc.tensor.matmul_mx(
-                    out=sums[key][:, m, at : at + width],
+                    out=sums[key][:, m, :],
                     lhsT=weights(nt)[0],
                     lhsT_scale=weights(nt)[1],
                     rhs=codes.bitcast(FP8X4),
                     rhs_scale=plane,
-                    start=(opening and m == 0),
-                    stop=(closing and not opening and m == len(tiles) - 1),
+                    start=(lone or opening and m == 0),
+                    stop=(lone or not opening and m == len(tiles) - 1),
                 )
 
         def wa_tile(nt):
@@ -288,6 +288,8 @@ def tile_list_absd_gelu_kernel(
 
         magnitude("0a", 0, 0, 0, P)
         magnitude("0b", 0, 0, P, PIECE)
+        for number, tiles in ((0, (0, 1)), (1, (2,))):
+            passes("warm%d" % number, number, tiles, wb_tile, part(z_q[1], 0, PIECE), True, lone=True)
         wb_passes("2lo", (0, 1), 2)
         wb_passes("2hi", (2, 3), 2)
         last = (("30", 0, (0,)), ("31", 7, (1,)), ("3hi", 1, (2, 3)))

@@ -94,8 +94,8 @@ def tile_list_absd_gelu_kernel(
         nc.sync.dma_start(out=wb_raw[:], in_=wb_rows)
         for t in range(1, PACK - 1):
             nc.sync.dma_start(out=z_planes[t][:], in_=zT_planes[t])
-        nc.sync.dma_start(out=wa_codes[:].bitcast(I32), in_=wa_words[0].bitcast(I32))
         nc.sync.dma_start(out=z_planes[PACK - 1][:], in_=zT_planes[PACK - 1])
+        nc.sync.dma_start(out=wa_codes[:].bitcast(I32), in_=wa_words[0].bitcast(I32))
         for q in range(4):
             nc.gpsimd.dma_start(
                 out=wa_plane[32 * q : 32 * q + 4, :].bitcast(I32),
@@ -183,7 +183,7 @@ def tile_list_absd_gelu_kernel(
 
         sums = {}
 
-        def passes(key, number, tiles, weights, moving, opening, lone=False):
+        def passes(key, number, tiles, weights, moving, opening):
             codes, plane = moving
             width = codes.shape[1]
             if opening:
@@ -195,8 +195,8 @@ def tile_list_absd_gelu_kernel(
                     lhsT_scale=weights(nt)[1],
                     rhs=codes.bitcast(FP8X4),
                     rhs_scale=plane,
-                    start=(lone or opening and m == 0),
-                    stop=(lone or not opening and m == len(tiles) - 1),
+                    start=(opening and m == 0),
+                    stop=(not opening and m == len(tiles) - 1),
                 )
 
         def wa_tile(nt):
@@ -233,9 +233,6 @@ def tile_list_absd_gelu_kernel(
         for key, number, tiles, lo in first:
             wa_passes(key, number, tiles, 0, lo, lo + P)
         wa_passes("0hi", 2, (2, 3), 0)
-        for c in (1, 2):
-            wa_passes("%dlo" % c, 1 + 2 * c, (0, 1), c)
-            wa_passes("%dhi" % c, 2 + 2 * c, (2, 3), c)
         for lo in (0, P):
             nc.vector.quantize_mx(
                 out=z0_codes[:, lo : lo + P].bitcast(FP8X4),
@@ -244,12 +241,12 @@ def tile_list_absd_gelu_kernel(
             )
         for key, number, tiles, lo in first:
             wb_passes(key, tiles, 0, lo, lo + P)
+        wa_passes("1lo", 3, (0, 1), 1)
         gather_z(late[:, 0, :], 2, 2 * PIECE, 3 * PIECE)
         wb_q.append(quantize("wb_hi", wb_grouped[:, N // 2 :, :], N // 2, tag="zg0"))
         wb_passes("0hi", (2, 3), 0)
         z_q[1] = quantize("z1", z_grouped[1], PIECE)
         wb_passes("1lo", (0, 1), 1)
-        wb_passes("1hi", (2, 3), 1)
         gather_z(late[:, 1, :], 3, 2 * PIECE, 3 * PIECE)
         late3 = keep.tile([P, 2, PIECE], F32, name="late3", tag="zg1", align_bytes=64)
         gather_z(late3[:, 0, :], 2, 3 * PIECE, J)
@@ -288,11 +285,18 @@ def tile_list_absd_gelu_kernel(
 
         magnitude("0a", 0, 0, 0, P)
         magnitude("0b", 0, 0, P, PIECE)
-        for number, tiles in ((0, (0, 1)), (1, (2,))):
-            passes("warm%d" % number, number, tiles, wb_tile, part(z_q[1], 0, PIECE), True, lone=True)
+        wa_passes("1hi", 0, (2, 3), 1)
+        wb_passes("1hi", (2, 3), 1)
+        wa_passes("2lo", 1, (0, 1), 2)
+        for lo in (0, P):
+            for nt in (0, 1):
+                gelu(nt, lo, lo + P)
+        store(0, 2, 0, PIECE)
+        magnitude("0hi", 0, 2)
+        wa_passes("2hi", 2, (2, 3), 2)
         wb_passes("2lo", (0, 1), 2)
         wb_passes("2hi", (2, 3), 2)
-        last = (("30", 0, (0,)), ("31", 7, (1,)), ("3hi", 1, (2, 3)))
+        last = (("30", 4, (0,)), ("31", 7, (1,)), ("3hi", 5, (2, 3)))
         for key, number, tiles in last:
             wa_passes(key, number, tiles, 3)
         for key, number, tiles in last:
@@ -308,8 +312,6 @@ def tile_list_absd_gelu_kernel(
         larger(3, "3hi", 0, 3, 2)
         larger(4, "3hi", 1, 3, 3)
 
-        finish(0, 0)
-        magnitude("0hi", 0, 2)
         magnitude("1lo", 1, 0)
         magnitude("1hi", 1, 2)
         finish(1, 0)

from contextlib import ExitStack

import concourse.mybir as mybir
from concourse.masks import make_identity

K, N, T, J = 512, 512, 2048, 1024
FLOPS = 2 * 2 * K * N * J
BYTES = 4 * (2 * K * T + 2 * 8 * J + K * N + N + N * J) + K * N // 2 + 16 * N + 2 * 2 * 8 * J

F32 = mybir.dt.float32
BF16 = mybir.dt.bfloat16
I32 = mybir.dt.int32
U32 = mybir.dt.uint32
U16 = mybir.dt.uint16
U8 = mybir.dt.uint8
FP8X4 = mybir.dt.float8_e4m3fn_x4
FP4X4 = mybir.dt.float4_e2m1fn_x4
ALU = mybir.AluOpType
ACT = mybir.ActivationFunctionType

P = 128
PACK = 4
HEADS = 8
GROUP = 16
TILES = N // P
PIECE = 256
CHUNKS = J // PIECE


def woven(src):
    return src.rearrange("p t (c i) -> p c t i", i=4)


def woven_out(dst):
    return dst.rearrange("p (c i) t -> p c t i", i=4)


def by_column(pair):
    return pair.rearrange("p t c -> p c t")


def tile_list_absd_gelu_kernel(
    tc, xT, wgt, zT, wgt2, wa_words, wa_scales, wb, b, offs, offs2, out
):
    nc = tc.nc
    with ExitStack() as ctx:
        keep = ctx.enter_context(tc.tile_pool(name="keep", bufs=1))
        over = ctx.enter_context(tc.tile_pool(name="over", bufs=1))
        psum = ctx.enter_context(tc.psum_pool(name="psum", bufs=1))

        def bank(i, shape, name):
            return psum.tile(shape, F32, name=name, tag="bank%d" % i)

        x_list = keep.tile([P, J // 16], U16, name="x_list")
        z_list = keep.tile([P, J // 16], U16, name="z_list")
        x_rows = keep.tile([P, P], F32, name="x_rows")
        z_rows = keep.tile([P, P], F32, name="z_rows")
        x_planes = [keep.tile([P, T], F32, name="x_plane%d" % t) for t in range(PACK)]
        z_planes = [keep.tile([P, T], F32, name="z_plane%d" % t) for t in range(PACK)]
        wa_codes = keep.tile([P, 2 * N], U8, name="wa_codes", align_bytes=64)
        wa_plane = keep.tile([P, N], U8, name="wa_plane", align_bytes=64)
        wb_raw = keep.tile([P, PACK, N], F32, name="wb_raw")
        bias = keep.tile([P, TILES], F32, name="bias")
        ident = keep.tile([P, P], F32, name="ident")
        warm_in = keep.tile([P, 8], F32, name="warm_in")
        warm_out = keep.tile([P, 8], F32, name="warm_out")

        nc.vector.memset(warm_in[:], 0.0)
        nc.scalar.activation(warm_out[:], warm_in[:], ACT.Gelu_apprx_tanh)
        make_identity(nc, ident[:])
        nc.vector.memset(x_rows[64:, :], 0.0)
        nc.vector.memset(z_rows[64:, :], 0.0)
        nc.vector.memset(wa_plane[:].bitcast(I32), 0)

        xT_planes = xT.rearrange("(p t) n -> t p n", t=PACK)
        zT_planes = zT.rearrange("(p t) n -> t p n", t=PACK)
        wb_rows = wb.rearrange("(p t) n -> p t n", t=PACK)

        def load_head_rows(rows, w):
            nc.sync.dma_start(
                out=rows[:64, :], in_=w.rearrange("p (a c j) -> (p a) c j", a=2, j=P)[0 : 2 * P : GROUP + 1]
            )

        load_head_rows(x_rows, wgt)
        nc.sync.dma_start(x_list[:], offs)
        nc.sync.dma_start(out=x_planes[0][:], in_=xT_planes[0])
        load_head_rows(z_rows, wgt2)
        nc.sync.dma_start(out=z_rows[64 : 64 + TILES, :], in_=b.rearrange("(c p) -> c p", p=P))
        nc.sync.dma_start(out=x_planes[1][:], in_=xT_planes[1])
        nc.sync.dma_start(z_list[:], offs2)
        nc.sync.dma_start(out=x_planes[2][:], in_=xT_planes[2])
        nc.sync.dma_start(out=x_planes[3][:], in_=xT_planes[3])
        nc.sync.dma_start(out=z_planes[0][:], in_=zT_planes[0])
        nc.sync.dma_start(out=wb_raw[:], in_=wb_rows)
        for t in range(1, PACK - 1):
            nc.sync.dma_start(out=z_planes[t][:], in_=zT_planes[t])
        nc.sync.dma_start(out=z_planes[PACK - 1][:], in_=zT_planes[PACK - 1])
        nc.sync.dma_start(out=wa_codes[:].bitcast(I32), in_=wa_words[0].bitcast(I32))
        for q in range(4):
            nc.gpsimd.dma_start(
                out=wa_plane[32 * q : 32 * q + 4, :].bitcast(I32),
                in_=wa_scales[0, 4 * q : 4 * q + 4, :].bitcast(I32),
            )

        x_weights = keep.tile([P, J], F32, name="x_weights")
        z_weights = keep.tile([P, J], F32, name="z_weights")

        def spread_weights(name, turned, first_bank, count, copy, weights, tags):
            by_head = turned[:, :64].rearrange("j (h c) -> j c h", h=HEADS)
            for i in range(HEADS // count):
                spread = keep.tile([P, count, HEADS, GROUP], F32, name="%s_spread%d" % (name, i), tag=tags[i], align_bytes=64)
                copy(
                    out=spread[:],
                    in_=by_head[:, count * i : count * (i + 1), :].unsqueeze(3).to_broadcast([P, count, HEADS, GROUP]),
                )
                back = bank(first_bank + i, [P, count, P], "%s_back%d" % (name, i))
                for c in range(count):
                    nc.tensor.transpose(back[:, c, :], spread[:, c].rearrange("j h r -> j (h r)"), ident[:])
                nc.scalar.copy(
                    out=weights[:, count * P * i : count * P * (i + 1)], in_=back[:].rearrange("p c j -> p (c j)")
                )

        x_turned = bank(0, [P, P], "x_turned")
        nc.tensor.transpose(x_turned[:], x_rows[:], ident[:])
        spread_weights("x", x_turned, 1, 2, nc.vector.tensor_copy, x_weights, ["s0", "s1", "s2", "s3"])
        z_turned = bank(4, [P, P], "z_turned")
        nc.tensor.transpose(z_turned[:], z_rows[:], ident[:])
        spread_weights("z", z_turned, 6, 4, nc.scalar.copy, z_weights, ["s2", "s3"])
        nc.scalar.copy(out=bias[:], in_=z_turned[:, 64 : 64 + TILES])

        def gather(dst, plane, places, weights, lo, hi):
            nc.vector.tensor_tensor(dst, plane[:].indirect(places[:, lo // 16 : hi // 16]), weights[:, lo:hi], ALU.mult)

        def gather_z(dst, t, lo, hi):
            gather(dst, z_planes[t], z_list, z_weights, lo, hi)

        def quantize(name, grouped, width, pool=keep, **place):
            codes = pool.tile([P, width], U32, name=name + "_codes", align_bytes=64, **place)
            plane = keep.tile([P, width], U8, name=name + "_plane", align_bytes=64)
            nc.vector.quantize_mx(
                out=codes[:].bitcast(FP8X4), scales=plane[:], in_=grouped.rearrange("p c t -> p (c t)")
            )
            return codes, plane

        xg = over.tile([P, PACK, J], F32, name="xg", align_bytes=64, offset=0)
        x_grouped = keep.tile([P, J, PACK], BF16, name="x_grouped", tag="s3", align_bytes=64)
        for t in range(PACK):
            step = (PIECE, J, J, J // 2)[t]
            for lo in range(0, J, step):
                gather(xg[:, t, lo : lo + step], x_planes[t], x_list, x_weights, lo, lo + step)
            if t % 2:
                for lo in range(0, J, J // 2):
                    nc.scalar.copy(
                        out=x_grouped[:, lo : lo + J // 2, t - 1 : t + 1],
                        in_=by_column(xg[:, t - 1 : t + 1, lo : lo + J // 2]),
                    )

        def quantize_x(c, count, offset):
            width = count * PIECE
            return quantize("x%d" % c, x_grouped[:, c * PIECE : c * PIECE + width, :], width, over, offset=offset)

        wb_grouped = keep.tile([P, N, PACK], BF16, name="wb_grouped", align_bytes=64)
        nc.scalar.activation(woven_out(wb_grouped[:]), woven(wb_raw[:]), ACT.Copy, scale=-1.0)

        zg0 = keep.tile([P, PIECE, PACK], BF16, name="zg0", align_bytes=64)
        zg1 = keep.tile([P, PIECE, PACK], BF16, name="zg1", align_bytes=64)
        zg23 = keep.tile([P, 2 * PIECE, PACK], BF16, name="zg23", align_bytes=64)
        z_grouped = [zg0[:], zg1[:], zg23[:, :PIECE, :], zg23[:, PIECE:, :]]
        z_first = keep.tile([P, 2, PIECE], F32, name="z_first", align_bytes=64)
        z_rest = keep.tile([P, 2, J - PIECE], F32, name="z_rest")
        gather_z(z_first[:, 0, :], 0, 0, PIECE)
        gather_z(z_rest[:, 0, :], 0, PIECE, J)
        x_early = quantize_x(0, 2, 0)
        x_q = {c: tuple(a[:, c * PIECE : (c + 1) * PIECE] for a in x_early) for c in range(2)}
        x_q[2] = quantize_x(2, 1, 8 * PIECE)
        gather_z(z_first[:, 1, :], 1, 0, PIECE)
        nc.scalar.copy(out=zg0[:, :, :2], in_=by_column(z_first[:]))
        gather_z(z_rest[:, 1, :PIECE], 1, PIECE, 2 * PIECE)
        nc.scalar.copy(out=zg1[:, :, :2], in_=by_column(z_rest[:, :, :PIECE]))
        gather_z(z_rest[:, 1, PIECE:], 1, 2 * PIECE, J)
        nc.scalar.copy(out=zg23[:, :, :2], in_=by_column(z_rest[:, :, PIECE:]))
        wb_q = [quantize("wb_lo", wb_grouped[:, : N // 2, :], N // 2, tag="z_first")]

        sums = {}

        def passes(key, number, tiles, weights, moving, opening):
            codes, plane = moving
            width = codes.shape[1]
            if opening:
                sums[key] = bank(number, [P, len(tiles), width], "sum_" + key)
            for m, nt in enumerate(tiles):
                nc.tensor.matmul_mx(
                    out=sums[key][:, m, :],
                    lhsT=weights(nt)[0],
                    lhsT_scale=weights(nt)[1],
                    rhs=codes.bitcast(FP8X4),
                    rhs_scale=plane,
                    start=(opening and m == 0),
                    stop=(not opening and m == len(tiles) - 1),
                )

        def wa_tile(nt):
            return wa_codes[:, 2 * P * nt : 2 * P * (nt + 1)].bitcast(FP4X4), wa_plane[:, P * nt : P * (nt + 1)]

        def wb_tile(nt):
            codes, plane = wb_q[nt // 2]
            at = P * (nt % 2)
            return codes[:, at : at + P].bitcast(FP8X4), plane[:, at : at + P]

        def part(q, lo, hi):
            return q[0][:, lo:hi], q[1][:, lo:hi]

        def wa_passes(key, number, tiles, c, lo=0, hi=PIECE):
            passes(key, number, tiles, wa_tile, part(x_q[c], lo, hi), True)

        def wb_passes(key, tiles, c, lo=0, hi=PIECE):
            passes(key, None, tiles, wb_tile, part(z_q[c], lo, hi), False)


        late01 = keep.tile([P, 2, 2 * PIECE], F32, name="late01", align_bytes=64)
        late = late01[:].rearrange("p t (c j) -> p (t c) j", c=2)[:, 0:4:3, :]
        gather_z(late01[:, 0, :], 2, 0, 2 * PIECE)
        for lo, hi in ((0, P), (P, PIECE), (PIECE, 2 * PIECE)):
            gather_z(late01[:, 1, lo:hi], 3, lo, hi)
        nc.scalar.copy(out=zg0[:, :P, 2:], in_=by_column(late01[:, :, :P]))
        nc.scalar.copy(out=zg0[:, P:, 2:], in_=by_column(late01[:, :, P:PIECE]))
        nc.scalar.copy(out=zg1[:, :, 2:], in_=by_column(late01[:, :, PIECE:]))

        z0_codes = keep.tile([P, PIECE], U32, name="z0_codes", align_bytes=64)
        z0_plane = keep.tile([P, PIECE], U8, name="z0_plane", align_bytes=64)
        z_q = {0: (z0_codes, z0_plane)}
        first = (("0a", 0, (0, 1), 0), ("0b", 1, (0, 1), P))
        for key, number, tiles, lo in first:
            wa_passes(key, number, tiles, 0, lo, lo + P)
        wa_passes("0hi", 2, (2, 3), 0)
        for lo in (0, P):
            nc.vector.quantize_mx(
                out=z0_codes[:, lo : lo + P].bitcast(FP8X4),
                scales=z0_plane[:, lo : lo + P],
                in_=zg0[:, lo : lo + P, :].rearrange("p c t -> p (c t)"),
            )
        for key, number, tiles, lo in first:
            wb_passes(key, tiles, 0, lo, lo + P)
        wa_passes("1lo", 3, (0, 1), 1)
        gather_z(late[:, 0, :], 2, 2 * PIECE, 3 * PIECE)
        wb_q.append(quantize("wb_hi", wb_grouped[:, N // 2 :, :], N // 2, tag="zg0"))
        wb_passes("0hi", (2, 3), 0)
        z_q[1] = quantize("z1", z_grouped[1], PIECE)
        wb_passes("1lo", (0, 1), 1)
        gather_z(late[:, 1, :], 3, 2 * PIECE, 3 * PIECE)
        late3 = keep.tile([P, 2, PIECE], F32, name="late3", tag="zg1", align_bytes=64)
        gather_z(late3[:, 0, :], 2, 3 * PIECE, J)
        nc.vector.tensor_copy(out=z_grouped[2][:, :, 2:], in_=by_column(late))
        gather_z(late3[:, 1, :], 3, 3 * PIECE, J)
        z_q[2] = quantize("z2", z_grouped[2], PIECE)
        nc.vector.tensor_copy(out=z_grouped[3][:, :, 2:], in_=by_column(late3[:]))
        x_q[3] = quantize("x3", x_grouped[:, 3 * PIECE :, :], PIECE, tag="late01")
        z_q[3] = quantize("z3", z_grouped[3], PIECE)

        out_tiles = out.rearrange("(nt p) j -> p nt j", p=P)
        mags = keep.tile([P, TILES, J], F32, name="mags")
        negs = keep.tile([P, 5, PIECE], F32, name="negs")
        done = keep.tile([P, TILES, J], F32, name="done")

        def magnitude(key, c, first, lo=0, hi=PIECE):
            count = sums[key].shape[1]
            nc.scalar.activation(mags[:, first : first + count, c * PIECE + lo : c * PIECE + hi], sums[key][:], ACT.Abs)

        def negate(slot, key, at):
            nc.vector.tensor_scalar(negs[:, slot, :], sums[key][:, at, :], -1.0, None, ALU.mult)

        def larger(slot, key, at, c, nt):
            nc.vector.tensor_tensor(mags[:, nt, c * PIECE : (c + 1) * PIECE], negs[:, slot, :], sums[key][:, at, :], ALU.max)

        def gelu(nt, lo, hi):
            nc.scalar.activation(done[:, nt, lo:hi], mags[:, nt, lo:hi], ACT.Gelu_apprx_tanh, bias=bias[:, nt : nt + 1])

        def store(first, count, lo, hi):
            nc.sync.dma_start(out=out_tiles[:, first : first + count, lo:hi], in_=done[:, first : first + count, lo:hi])

        def finish(c, first):
            gelu(first, c * PIECE, (c + 1) * PIECE)
            gelu(first + 1, c * PIECE, (c + 1) * PIECE)
            store(first, 2, c * PIECE, (c + 1) * PIECE)

        magnitude("0a", 0, 0, 0, P)
        magnitude("0b", 0, 0, P, PIECE)
        wa_passes("1hi", 0, (2, 3), 1)
        wb_passes("1hi", (2, 3), 1)
        wa_passes("2lo", 1, (0, 1), 2)
        for lo in (0, P):
            for nt in (0, 1):
                gelu(nt, lo, lo + P)
        store(0, 2, 0, PIECE)
        magnitude("0hi", 0, 2)
        wa_passes("2hi", 2, (2, 3), 2)
        wb_passes("2lo", (0, 1), 2)
        wb_passes("2hi", (2, 3), 2)
        last = (("30", 4, (0,)), ("31", 7, (1,)), ("3hi", 5, (2, 3)))
        for key, number, tiles in last:
            wa_passes(key, number, tiles, 3)
        for key, number, tiles in last:
            wb_passes(key, tiles, 3)
        negate(0, "2hi", 0)
        negate(1, "2hi", 1)
        larger(0, "2hi", 0, 2, 2)
        larger(1, "2hi", 1, 2, 3)
        negate(2, "31", 0)
        negate(3, "3hi", 0)
        larger(2, "31", 0, 3, 1)
        negate(4, "3hi", 1)
        larger(3, "3hi", 0, 3, 2)
        larger(4, "3hi", 1, 3, 3)

        magnitude("1lo", 1, 0)
        magnitude("1hi", 1, 2)
        finish(1, 0)
        for nt in (2, 3):
            if nt == TILES - 1:
                magnitude("2lo", 2, 0)
            gelu(nt, 0, 2 * PIECE)
            store(nt, 1, 0, 2 * PIECE)
        finish(2, 0)
        magnitude("30", 3, 0)
        finish(2, 2)
        finish(3, 0)
        for nt in (2, 3):
            gelu(nt, 3 * PIECE, J)
            store(nt, 1, 3 * PIECE, J)
